import numpy as np
import ml_dtypes


def mxq(x, axis, fmt="e4m3"):
    dtype, down = {"e4m3": (ml_dtypes.float8_e4m3fn, 7), "e5m2": (ml_dtypes.float8_e5m2, 14)}[fmt]
    v = np.moveaxis(np.asarray(x, np.float32).astype(ml_dtypes.bfloat16).astype(np.float64), axis, -1)
    blocks = v.reshape(v.shape[:-1] + (-1, 32))
    amax = np.abs(blocks).max(-1, keepdims=True)
    byte = np.maximum(np.where(amax > 0, np.frexp(amax)[1] - 1 + 127, 0) - down, 1)
    scale = np.exp2(byte - 127.0)
    codes = (blocks / scale).astype(np.float32).astype(dtype).astype(np.float64)
    return np.moveaxis((codes * scale).reshape(v.shape), -1, axis)


WIDE = False


def mx_kscale(k):
    if not WIDE:
        return np.ones(k)
    levels = np.array([10, -10, 5, -5, 0])
    if k % 512:
        return np.exp2(np.random.permutation(np.resize(levels, k // 32))).repeat(32)
    a = np.empty((k // 512, 16))
    for p in range(k // 512):
        a[p, :8] = np.random.permutation(np.resize(levels, 8))
        for g in range(8):
            far = levels[np.abs(levels - a[p, g]) >= 10]
            a[p, g + 8] = far[np.random.randint(len(far))]
    return np.exp2(a.ravel()).repeat(32)


BF16 = ml_dtypes.bfloat16


def bf(x):
    return np.asarray(x, np.float32).astype(BF16)


def f64(x):
    return np.asarray(x).astype(np.float64)


T, S, D, E, H = 2048, 512, 1024, 1024, 8

EPS = 1e-6
BASE = 10000.0


def draw0():
    s, t, u = mx_kscale(T), mx_kscale(D), mx_kscale(S)
    half = E // H // 2
    pos = np.random.uniform(0.0, T, S)
    angle = pos[:, None] * BASE ** (-np.arange(half) / half)[None, :]
    return {"x": bf(np.random.standard_normal((T, D)) * s[:, None]),
            "pool": bf(np.random.standard_normal((S, T)) / np.sqrt(T) / s),
            "slot_emb": bf(0.3 * np.random.standard_normal((S, D))),
            "gain": bf((1.0 + 0.1 * np.random.standard_normal(D)) * t),
            "slot_scale": bf((1.0 + 0.1 * np.random.standard_normal(S)) * u),
            "w_up": bf(np.random.standard_normal((D, 2 * E)) / np.sqrt(D) / t[:, None]),
            "tau": bf((1.0 + 0.1 * np.random.standard_normal(S)) / u),
            "b_up": bf(0.3 * np.random.standard_normal(2 * E)),
            "cos_t": bf(np.cos(angle)),
            "sin_t": bf(np.sin(angle)),
            "unpool": bf(np.random.standard_normal((T, S)) / np.sqrt(S) / u),
            "restore": bf((1.0 + 0.1 * np.random.standard_normal(D)) / t),
            "b_rec": bf(0.3 * np.random.standard_normal(D))}


def rotate(k, c, s):
    half = E // H // 2
    kh = k.reshape(S, H, 2, half)
    k1, k2 = kh[:, :, 0, :], kh[:, :, 1, :]
    c, s = c[:, None, :], s[:, None, :]
    return np.stack([k1 * c - k2 * s, k1 * s + k2 * c], axis=2).reshape(S, E)


def core(x, pool, slot_emb, gain, slot_scale, w_up, tau, b_up, cos_t, sin_t, unpool, restore, b_rec):
    c = (mxq(f64(pool), 1, "e4m3") @ mxq(f64(x), 0, "e4m3")) + f64(slot_emb)
    r = 1.0 / np.sqrt(np.mean(c * c, axis=1, keepdims=True) + EPS)
    z = c * r * f64(gain)[None, :] * f64(slot_scale)[:, None]
    kv = mxq(z, 1, "e4m3") @ mxq(f64(w_up), 0, "e4m3")
    kv = kv * f64(tau)[:, None] + f64(b_up)[None, :]
    keys = rotate(kv[:, :E], f64(cos_t), f64(sin_t))
    values = kv[:, E:]
    rec = mxq(f64(unpool), 1, "e4m3") @ mxq(z, 0, "e4m3")
    rec = rec * f64(restore)[None, :] + f64(b_rec)[None, :]
    return keys, values, rec


def e4m3fn_bytes(y):
    return np.clip(np.asarray(y, np.float64), -448.0, 448.0).astype(np.float32).astype(ml_dtypes.float8_e4m3fn).view(np.uint8)


def e4m3fn_values(b):
    return np.asarray(b, np.uint8).view(ml_dtypes.float8_e4m3fn).astype(np.float64)


def setup_inputs():
    d = draw0()
    x0 = np.asarray(d['x']).astype(np.float64)
    s = (np.max(np.abs(x0), axis=(1,), keepdims=True) / 448.0).astype(np.float32)
    out = {}
    for k, v in d.items():
        if k == 'x':
            out['x_bytes'] = e4m3fn_bytes(x0 / s.astype(np.float64))
            out['x_scale'] = s
        else:
            out[k] = v
    return out


def reference(x_bytes, x_scale, pool, slot_emb, gain, slot_scale, w_up, tau, b_up, cos_t, sin_t, unpool, restore, b_rec):
    return core(e4m3fn_values(x_bytes) * x_scale.astype(np.float64), pool, slot_emb, gain, slot_scale, w_up, tau, b_up, cos_t, sin_t, unpool, restore, b_rec)

@@ -1,0 +1,621 @@
+from contextlib import ExitStack
+
+import concourse.mybir as mybir
+from concourse.masks import make_identity
+
+T, S, D, E = 2048, 512, 1024, 1024
+HALF = 64
+EPS = 1e-6
+P = 128
+FLOPS = 3 * 2 * S * T * D
+
+F32 = mybir.dt.float32
+BF16 = mybir.dt.bfloat16
+U32 = mybir.dt.uint32
+U8 = mybir.dt.uint8
+FP8 = mybir.dt.float8_e4m3fn
+X4 = mybir.dt.float8_e4m3fn_x4
+ALU = mybir.AluOpType
+ACT = mybir.ActivationFunctionType
+
+
+def span(start, width):
+    return slice(start, start + width)
+
+
+def words(ap):
+    return ap.bitcast(F32)
+
+
+def tile_cache_pool_upproject_f6_kernel(
+    tc, x_bytes, x_scale, pool, slot_emb, gain, slot_scale, w_up, tau, b_up,
+    cos_t, sin_t, unpool, restore, b_rec, keys, values, rec,
+):
+    nc = tc.nc
+    with ExitStack() as ctx:
+        keep = ctx.enter_context(tc.tile_pool(name="keep", bufs=1))
+        work = ctx.enter_context(tc.tile_pool(name="work", bufs=1))
+        psum = ctx.enter_context(tc.psum_pool(name="psum", bufs=8))
+        ctx.enter_context(tc.manual_schedule())
+
+        def bank(shape, label, dtype=F32):
+            return psum.tile(shape, dtype, tag="bank", name=label)
+
+        def big(shape, dtype, label):
+            return work.tile(shape, dtype, tag="s8", name=label, bufs=5, align_bytes=64)
+
+        def small(shape, dtype, label):
+            return work.tile(shape, dtype, tag="s4", name=label, bufs=7, align_bytes=64)
+
+        def loaded(shape, label):
+            return work.tile(shape, BF16, tag="ld8", name=label, bufs=6, align_bytes=64)
+
+        xsc = keep.tile([P, 4, 4], F32, name="xsc")
+        nc.scalar.dma_start(out=xsc[:], in_=x_scale.rearrange("(g p t) o -> p g (t o)", p=P, t=4))
+        x_view = x_bytes.rearrange("(g p t) d -> g p t d", p=P, t=4)
+        pool_view = pool.rearrange("(m t) k -> m t k", t=4)
+        xb = {}
+        pr = []
+        for g in range(4):
+            for th in range(2):
+                xb_g = keep.tile([P, 2, D], U8, name="xb%d%d" % (g, th), align_bytes=64)
+                nc.sync.dma_start(out=xb_g[:], in_=x_view[g][:, span(2 * th, 2), :])
+                xb[g, th] = xb_g
+            if g % 2 == 0:
+                pr_g = loaded([P, 4, 1024], "pr")
+                pr.append(pr_g)
+            nc.sync.dma_start(out=pr[g // 2][:, :, span(512 * (g % 2), 512)], in_=pool_view[:, :, span(512 * g, 512)])
+        w_view = w_up.rearrange("(g p t) n -> g p t n", p=P, t=4)
+        wr = {}
+
+        def load_w(q):
+            w_q = loaded([P, 4, 1024], "wr")
+            nc.sync.dma_start(out=w_q[:], in_=w_view[q % 2][:, :, span(1024 * (q // 2), 1024)])
+            wr[q] = w_q
+
+        load_w(0)
+        emb = keep.tile([P, 4, D], BF16, name="emb")
+        nc.sync.dma_start(out=emb[:], in_=slot_emb.rearrange("(m t) d -> m t d", t=4))
+        gain_b = keep.tile([P, D], BF16, name="gain_b")
+        nc.sync.dma_start(out=gain_b[:], in_=gain.partition_broadcast(P))
+        load_w(1)
+        un_view = unpool.rearrange("(p a) s -> p a s", a=16)
+        un = []
+        for i in range(2):
+            un_i = loaded([P, 8, S], "un")
+            nc.sync.dma_start(out=un_i[:], in_=un_view[:, span(8 * i, 8), :])
+            un.append(un_i)
+        rest_b = keep.tile([P, D], BF16, name="rest_b")
+        nc.sync.dma_start(out=rest_b[:], in_=restore.partition_broadcast(P))
+        brec_b = keep.tile([P, D], BF16, name="brec_b")
+        nc.sync.dma_start(out=brec_b[:], in_=b_rec.partition_broadcast(P))
+        load_w(2)
+        load_w(3)
+        bup_b = keep.tile([P, 2 * E], BF16, name="bup_b")
+        nc.sync.dma_start(out=bup_b[:], in_=b_up.partition_broadcast(P))
+
+        one = keep.tile([P, 1], F32, name="one")
+        nc.vector.memset(one[:], 1.0)
+        rows = keep.tile([P, P], BF16, name="rows")
+        nc.vector.memset(rows[:], 0.0)
+        warm = keep.tile([P, 1], F32, name="warm")
+        nc.scalar.activation(out=warm[:], in_=one[:], func=ACT.Sqrt)
+        ident = keep.tile([P, P], F32, name="ident")
+        make_identity(nc, ident[:])
+        ident16 = keep.tile([P, P], BF16, name="ident16")
+        make_identity(nc, ident16[:])
+        nc.gpsimd.dma_start(out=rows[0:8, :], in_=restore.rearrange("(j p) -> j p", p=P))
+        nc.gpsimd.dma_start(out=rows[8:16, :], in_=b_rec.rearrange("(j p) -> j p", p=P))
+        ss_b = keep.tile([P, 4], BF16, name="ss_b")
+        nc.gpsimd.dma_start(out=ss_b[:], in_=slot_scale.rearrange("(m t) -> m t", t=4))
+        tau_b = keep.tile([P, 4], BF16, name="tau_b")
+        nc.gpsimd.dma_start(out=tau_b[:], in_=tau.rearrange("(m t) -> m t", t=4))
+        cos_b = keep.tile([P, 4, HALF], BF16, name="cos_b")
+        nc.gpsimd.dma_start(out=cos_b[:], in_=cos_t.rearrange("(m t) d -> m t d", t=4))
+        sin_b = keep.tile([P, 4, HALF], BF16, name="sin_b")
+        nc.gpsimd.dma_start(out=sin_b[:], in_=sin_t.rearrange("(m t) d -> m t d", t=4))
+        cols = keep.tile([P, 16], F32, name="cols")
+        ssin = keep.tile([P, 4, 2, HALF], BF16, name="ssin")
+
+        def column_constants():
+            turned = bank([P, P], "turned", BF16)
+            nc.tensor.transpose(turned[:], rows[:], ident16[:])
+            nc.vector.tensor_copy(out=cols[:], in_=turned[:, 0:16])
+
+        tau_f = keep.tile([P, 4], F32, name="tau_f")
+
+        def signed_sine():
+            nc.vector.tensor_copy(out=tau_f[:], in_=tau_b[:])
+            nc.vector.tensor_scalar(out=ssin[:, :, 0, :], in0=sin_b[:], scalar1=-1.0, scalar2=None, op0=ALU.mult)
+            nc.vector.tensor_copy(out=ssin[:, :, 1, :], in_=sin_b[:])
+
+        def interleave(engine_copy, dst, src):
+            engine_copy(
+                out=dst.rearrange("p (c i) t -> p c t i", i=4),
+                in_=src.rearrange("p t (c i) -> p c t i", i=4),
+            )
+
+        def quantize(codes, scales, values4):
+            nc.vector.quantize_mx(out=codes.bitcast(X4), scales=scales, in_=values4)
+
+        xw, xi, xq, xs, pi, pq, ps = {}, {}, {}, {}, {}, {}, {}
+        turned_pool, acc = {}, {}
+
+        def x_widen(g, t, vector, at=0, width=D):
+            if g not in xw:
+                xw_g = big([P, 4, D], BF16, "xw")
+                xw[g] = xw_g
+            c = span(at, width)
+            src = xb[g, t // 2][:, t % 2, c].bitcast(FP8)
+            scale = xsc[:, g, t : t + 1]
+            if vector:
+                nc.vector.tensor_scalar(out=xw[g][:, t, c], in0=src, scalar1=scale, scalar2=None, op0=ALU.mult)
+            else:
+                nc.scalar.activation(out=xw[g][:, t, c], in_=src, func=ACT.Copy, scale=scale)
+
+        def x_interleave(g, at, width, vector=True):
+            if g not in xi:
+                xi_g = big([P, D, 4], BF16, "xi")
+                xi[g] = xi_g
+            c = span(at, width)
+            interleave(nc.vector.tensor_copy if vector else nc.scalar.copy, xi[g][:, c, :], xw[g][:, :, c])
+
+        def x_quantize(g, h):
+            if g not in xq:
+                xq_g = work.tile([P, 1024], U32, tag="codes", name="xq", bufs=6, align_bytes=64)
+                xs_g = work.tile([P, 1024], U8, tag="scales", name="xs", bufs=6, align_bytes=64)
+                xq[g], xs[g] = xq_g, xs_g
+            c = span(512 * h, 512)
+            quantize(xq[g][:, c], xs[g][:, c], xi[g][:, c, :].rearrange("p c j -> p (c j)"))
+
+        def pool_turn(g, hp):
+            pw = words(pr[g // 2][:].rearrange("m t k -> m (t k)"))
+            tb = bank([P, 2, 2, P], "tb")
+            turned_pool[g, hp] = tb
+            for i in range(2):
+                base = (2 * hp + i) * 512 + 256 * (g % 2)
+                for u in range(2):
+                    nc.tensor.transpose(tb[:, i, u, :], pw[:, base + u : base + 256 : 2], ident[:])
+
+        def pool_copy(g, hp, vector=False):
+            if g not in pi:
+                pi_g = small([P, S, 4], BF16, "pi")
+                pi[g] = pi_g
+            w = words(pi[g][:].rearrange("p c j -> p (c j)")).rearrange("p (t m u) -> p t m u", t=4, u=2)
+            fn = nc.vector.tensor_copy if vector else nc.scalar.copy
+            fn(out=w[:, span(2 * hp, 2)], in_=turned_pool[g, hp][:].rearrange("p t u m -> p t m u"))
+
+        def pool_quantize(g):
+            pq_g = keep.tile([P, S], U32, name="pq%d" % g, align_bytes=64)
+            ps_g = keep.tile([P, S], U8, name="ps%d" % g, align_bytes=64)
+            quantize(pq_g[:], ps_g[:], pi[g][:].rearrange("p c j -> p (c j)"))
+            pq[g], ps[g] = pq_g, ps_g
+
+        def pooled(tp, g, h):
+            if g == 0:
+                a_t = bank([P, 512], "acc")
+                acc[tp, h] = a_t
+            nc.tensor.matmul_mx(
+                out=acc[tp, h][:],
+                lhsT=pq[g][:, span(P * tp, P)].bitcast(X4), lhsT_scale=ps[g][:, span(P * tp, P)],
+                rhs=xq[g][:, span(512 * h, 512)].bitcast(X4), rhs_scale=xs[g][:, span(512 * h, 512)],
+                start=(g == 0), stop=(g == 3),
+            )
+
+        zb = keep.tile([P, 4, D], BF16, name="zb", align_bytes=64)
+        zi = {}
+        c_f, zt, zti, ztq, zts = {}, {}, {}, {}, {}
+
+        def c_add(tp, h):
+            if h == 0:
+                c_t = small([P, D], F32, "c")
+                c_f[tp] = c_t
+            n = span(512 * h, 512)
+            nc.vector.tensor_tensor(out=c_f[tp][:, n], in0=acc[tp, h][:], in1=emb[:, tp, n], op=ALU.add)
+
+        ssum = keep.tile([P, 4], F32, name="ssum")
+        ms = keep.tile([P, 4], F32, name="ms")
+        rt = keep.tile([P, 4], F32, name="rt")
+        rr = keep.tile([P, 4], F32, name="rr")
+        rs = keep.tile([P, 4], F32, name="rs")
+
+        def c_square(tp):
+            sq = small([P, D], BF16, "sq")
+            nc.scalar.activation(out=sq[:], in_=c_f[tp][:], func=ACT.Square, accum_out=ssum[:, tp : tp + 1])
+
+        def c_mean(pair):
+            n = span(2 * pair, 2)
+            nc.vector.tensor_scalar(out=ms[:, n], in0=ssum[:, n], scalar1=1.0 / D, scalar2=EPS, op0=ALU.mult, op1=ALU.add)
+
+        def c_root(pair):
+            n = span(2 * pair, 2)
+            nc.scalar.activation(out=rt[:, n], in_=ms[:, n], func=ACT.Sqrt)
+
+        def c_scale(pair):
+            n = span(2 * pair, 2)
+            nc.vector.reciprocal(out=rr[:, n], in_=rt[:, n])
+            nc.vector.tensor_tensor(out=rs[:, n], in0=rr[:, n], in1=ss_b[:, n], op=ALU.mult)
+
+        def z_make(tp):
+            nc.vector.scalar_tensor_tensor(out=zb[:, tp, :], in0=c_f[tp][:], scalar=rs[:, tp : tp + 1], in1=gain_b[:], op0=ALU.mult, op1=ALU.mult)
+
+        def z_turn(tp):
+            zw = words(zb[:, tp, :])
+            zt_t = bank([P, 2, 2, P], "ztb")
+            for g in range(2):
+                for u in range(2):
+                    nc.tensor.transpose(zt_t[:, g, u, :], zw[:, 256 * g + u : 256 * g + 256 : 2], ident[:])
+            zt[tp] = zt_t
+
+        def z_copy(tp):
+            z_t = small([P, 2, P, 4], BF16, "zti")
+            nc.scalar.copy(
+                out=words(z_t[:].rearrange("p g m j -> p (g m j)")).rearrange("p (g m u) -> p g m u", g=2, u=2),
+                in_=zt[tp][:].rearrange("p g u m -> p g m u"),
+            )
+            zti[tp] = z_t
+
+        def z_quantize(tp):
+            ztq_t = keep.tile([P, 2, P], U32, name="ztq%d" % tp, align_bytes=64)
+            zts_t = keep.tile([P, 2, P], U8, name="zts%d" % tp, align_bytes=64)
+            quantize(ztq_t[:].rearrange("p g m -> p (g m)"), zts_t[:].rearrange("p g m -> p (g m)"), zti[tp][:].rearrange("p g m j -> p (g m j)"))
+            ztq[tp], zts[tp] = ztq_t, zts_t
+
+        zq = keep.tile([P, D], U32, name="zq", align_bytes=64)
+        zs = keep.tile([P, D], U8, name="zs", align_bytes=64)
+
+        def zi_interleave(at, width, vector=True):
+            if 0 not in zi:
+                zi_t = big([P, D, 4], BF16, "zi")
+                zi[0] = zi_t
+            c = span(at, width)
+            interleave(nc.vector.tensor_copy if vector else nc.scalar.copy, zi[0][:, c, :], zb[:, :, c])
+
+        def zi_quantize(at, width):
+            c = span(at, width)
+            quantize(zq[:, c], zs[:, c], zi[0][:, c, :].rearrange("p c j -> p (c j)"))
+
+        uq = keep.tile([P, T], U32, name="uq", align_bytes=64)
+        us = keep.tile([P, T], U8, name="us", align_bytes=64)
+        ui, turned_un = {}, {}
+
+        def un_turn(b, hp):
+            uw = words(un[b // 2][:].rearrange("p a s -> p (a s)"))
+            tb = bank([P, 2, 2, P], "tu")
+            turned_un[b, hp] = tb
+            for i in range(2):
+                base = (4 * (b % 2) + 2 * hp + i) * 256
+                for u in range(2):
+                    nc.tensor.transpose(tb[:, i, u, :], uw[:, base + u : base + 256 : 2], ident[:])
+
+        def un_copy(b, hp, vector=False):
+            if b not in ui:
+                ui_b = small([P, 4, P, 4], BF16, "ui")
+                ui[b] = ui_b
+            w = words(ui[b][:].rearrange("p a m j -> p (a m j)")).rearrange("p (a m u) -> p a m u", a=4, u=2)
+            fn = nc.vector.tensor_copy if vector else nc.scalar.copy
+            fn(out=w[:, span(2 * hp, 2)], in_=turned_un[b, hp][:].rearrange("p a u m -> p a m u"))
+
+        def un_quantize(b):
+            c = span(512 * b, 512)
+            quantize(uq[:, c], us[:, c], ui[b][:].rearrange("p a m j -> p (a m j)"))
+
+        wp, wi, wq, ws = {}, {}, {}, {}
+
+        def w_weave(b):
+            q, c = b // 4, 256 * (b % 4)
+            wp_b = bank([P, 256, 4], "wp", BF16)
+            wp[b] = wp_b
+            for n in range(2):
+                nc.tensor.matmul(
+                    out=wp_b[:, span(128 * n, 128), :].rearrange("p c t -> p (c t)"), lhsT=ident16[:],
+                    rhs=wr[q][:, :, span(c + 128 * n, 128)].rearrange("p t c -> p c t"), start=True, stop=True,
+                )
+
+        def w_tile(q):
+            if q not in wi:
+                wi_q = big([P, 1024, 4], BF16, "wi")
+                wi[q] = wi_q
+
+        def w_copy(b, vector=False):
+            q = b // 4
+            w_tile(q)
+            fn = nc.vector.tensor_copy if vector else nc.scalar.copy
+            fn(out=wi[q][:, span(256 * (b % 4), 256), :], in_=wp[b][:])
+
+        def w_direct(b, vector=True):
+            q, c = b // 4, span(256 * (b % 4), 256)
+            w_tile(q)
+            interleave(nc.vector.tensor_copy if vector else nc.scalar.copy, wi[q][:, c, :], wr[q][:, :, c])
+
+        def w_quantize(q, h):
+            if q not in wq:
+                wq_q = work.tile([P, 1024], U32, tag="codes", name="wq", bufs=6, align_bytes=64)
+                ws_q = work.tile([P, 1024], U8, tag="scales", name="ws", bufs=6, align_bytes=64)
+                wq[q], ws[q] = wq_q, ws_q
+            c = span(512 * h, 512)
+            quantize(wq[q][:, c], ws[q][:, c], wi[q][:, c, :].rearrange("p c j -> p (c j)"))
+
+        rec_view = rec.rearrange("(p a) d -> p a d", a=16)
+        pa, ro = {}, {}
+
+        def a_mm(a, h):
+            pa_t = bank([P, 512], "pa")
+            pa[a, h] = pa_t
+            n = span(512 * h, 512)
+            nc.tensor.matmul_mx(
+                out=pa_t[:], lhsT=uq[:, span(P * a, P)].bitcast(X4), lhsT_scale=us[:, span(P * a, P)],
+                rhs=zq[:, n].bitcast(X4), rhs_scale=zs[:, n], start=True, stop=True,
+            )
+
+        def a_mul(a, h):
+            ro_a = work.tile([P, 512], F32, tag="s2", name="ro", bufs=8)
+            ro[a, h] = ro_a
+            nc.vector.tensor_tensor(out=ro_a[:], in0=pa[a, h][:], in1=rest_b[:, span(512 * h, 512)], op=ALU.mult)
+
+        def a_add(a, h, vector=False):
+            (nc.vector if vector else nc.gpsimd).tensor_tensor(out=ro[a, h][:], in0=ro[a, h][:], in1=brec_b[:, span(512 * h, 512)], op=ALU.add)
+
+        def a_store(a, h):
+            nc.sync.dma_start(out=rec_view[:, a, span(512 * h, 512)], in_=ro[a, h][:])
+
+        pt, rt_s, pc, rq = {}, {}, {}, {}
+
+        def t_mm(b, j):
+            pt_t = bank([P, 512], "pt")
+            pt[b, j] = pt_t
+            f, c = span(P * j, P), span(512 * b, 512)
+            nc.tensor.matmul_mx(
+                out=pt_t[:], lhsT=zq[:, f].bitcast(X4), lhsT_scale=zs[:, f],
+                rhs=uq[:, c].bitcast(X4), rhs_scale=us[:, c], start=True, stop=True,
+            )
+
+        def t_affine(b, j):
+            r_t = work.tile([P, 512], F32, tag="s2", name="rt_s", bufs=8)
+            nc.scalar.activation(out=r_t[:], in_=pt[b, j][:], func=ACT.Identity, scale=cols[:, j : j + 1], bias=cols[:, 8 + j : 9 + j])
+            rt_s[b, j] = r_t
+
+        def t_turn(b, j):
+            pc_t = bank([P, 4, P], "pc")
+            for i in range(4):
+                nc.tensor.transpose(pc_t[:, i, :], rt_s[b, j][:, span(P * i, P)], ident[:])
+            pc[b, j] = pc_t
+
+        def t_copy(b, j, vector=False):
+            key = (b, j // 4)
+            if key not in rq:
+                rq_t = big([P, 4, 512], F32, "rq")
+                rq[key] = rq_t
+            fn = nc.vector.tensor_copy if vector else nc.scalar.copy
+            fn(out=rq[key][:, :, span(P * (j % 4), P)], in_=pc[b, j][:])
+
+        def t_store(b, jh):
+            nc.sync.dma_start(out=rec_view[:, span(4 * b, 4), span(512 * jh, 512)], in_=rq[b, jh][:])
+
+        keys_view = keys.rearrange("(m t) e -> m t e", t=4)
+        values_view = values.rearrange("(m t) e -> m t e", t=4)
+        pk, kv, m1, m2 = {}, {}, {}, {}
+
+        def kv_mm(tp, h, n):
+            pk_t = bank([P, 512], "pk")
+            pk[tp, h, n] = pk_t
+            c = span(512 * n, 512)
+            for g in range(2):
+                q = 2 * h + g
+                nc.tensor.matmul_mx(
+                    out=pk_t[:], lhsT=ztq[tp][:, g, :].bitcast(X4), lhsT_scale=zts[tp][:, g, :],
+                    rhs=wq[q][:, c].bitcast(X4), rhs_scale=ws[q][:, c], start=(g == 0), stop=(g == 1),
+                )
+
+        def kv_scale(tp, h, n):
+            if (tp, h) not in kv:
+                kv_t = small([P, 1024], F32, "kv")
+                kv[tp, h] = kv_t
+            c = span(512 * n, 512)
+            nc.vector.scalar_tensor_tensor(
+                out=kv[tp, h][:, c], in0=pk[tp, h, n][:], scalar=tau_b[:, tp : tp + 1],
+                in1=bup_b[:, span(1024 * h + 512 * n, 512)], op0=ALU.mult, op1=ALU.add,
+            )
+
+        def v_tau(tp, n):
+            if (tp, 1) not in kv:
+                kv_t = small([P, 1024], F32, "kv")
+                kv[tp, 1] = kv_t
+            nc.scalar.activation(out=kv[tp, 1][:, span(512 * n, 512)], in_=pk[tp, 1, n][:], func=ACT.Copy, scale=tau_f[:, tp : tp + 1])
+
+        def v_bias(tp, n):
+            c = span(512 * n, 512)
+            nc.gpsimd.tensor_tensor(out=kv[tp, 1][:, c], in0=kv[tp, 1][:, c], in1=bup_b[:, span(1024 + 512 * n, 512)], op=ALU.add)
+
+        def k_cos(tp, vector=False):
+            m1_t = small([P, 1024], F32, "m1")
+            m1[tp] = m1_t
+            (nc.vector if vector else nc.gpsimd).tensor_tensor(
+                out=m1_t[:].rearrange("p (h d) -> p h d", d=HALF), in0=kv[tp, 0][:].rearrange("p (h d) -> p h d", d=HALF),
+                in1=cos_b[:, tp, :].unsqueeze(1).to_broadcast([P, 16, HALF]), op=ALU.mult,
+            )
+
+        def k_sin(tp, s, vector=True):
+            if s == 0:
+                m2_t = small([P, 1024], F32, "m2")
+                m2[tp] = m2_t
+            kh = kv[tp, 0][:].rearrange("p (h s d) -> p h s d", s=2, d=HALF)
+            mh = m2[tp][:].rearrange("p (h s d) -> p h s d", s=2, d=HALF)
+            (nc.vector if vector else nc.gpsimd).tensor_tensor(
+                out=mh[:, :, s, :], in0=kh[:, :, 1 - s, :],
+                in1=ssin[:, tp, s, :].unsqueeze(1).to_broadcast([P, 8, HALF]), op=ALU.mult,
+            )
+
+        def k_add(tp, vector=True):
+            (nc.vector if vector else nc.gpsimd).tensor_tensor(out=m1[tp][:], in0=m1[tp][:], in1=m2[tp][:], op=ALU.add)
+
+        def k_store(tp):
+            nc.sync.dma_start(out=keys_view[:, tp, :], in_=m1[tp][:])
+
+        def v_store(tp):
+            nc.sync.dma_start(out=values_view[:, tp, :], in_=kv[tp, 1][:])
+
+        for h in range(2):
+            for t in range(4):
+                x_widen(0, t, t % 2 == 1, 512 * h, 512)
+        for hp in range(2):
+            pool_turn(0, hp)
+        for hp in range(2):
+            pool_copy(0, hp)
+        for g in range(4):
+            nxt = g + 1
+            if nxt < 4:
+                for hp in range(2):
+                    pool_turn(nxt, hp)
+                for t in range(3 if nxt in (1, 3) else 4):
+                    x_widen(nxt, t, False)
+            x_interleave(g, 0, 512)
+            pool_quantize(g)
+            if g < 3:
+                x_interleave(g, 512, 512)
+            else:
+                x_interleave(g, 768, 256, False)
+                x_interleave(g, 512, 256)
+            x_quantize(g, 0)
+            if nxt in (1, 3):
+                x_widen(nxt, 3, True)
+            x_quantize(g, 1)
+            if nxt < 4:
+                for hp in range(2):
+                    pool_copy(nxt, hp)
+            if g == 3:
+                for k in range(3):
+                    for h in range(2):
+                        pooled(3, k, h)
+            for tp in range(4 if g == 3 else 3):
+                for h in range(2):
+                    pooled(tp, g, h)
+            if 1 <= g < 3:
+                w_weave(g - 1)
+                w_copy(g - 1)
+
+        for tp in range(4):
+            c_add(tp, 0)
+            c_add(tp, 1)
+            if tp == 0:
+                un_turn(0, 0)
+                un_turn(0, 1)
+            if tp == 1:
+                w_weave(2)
+                w_weave(3)
+        for tp in range(3):
+            c_square(tp)
+        c_mean(0)
+        w_quantize(0, 0)
+        c_root(0)
+        c_square(3)
+        c_scale(0)
+        z_make(0)
+        z_turn(0)
+        un_copy(0, 0)
+        c_mean(1)
+        c_root(1)
+        z_make(1)
+        z_turn(1)
+        un_copy(0, 1)
+        c_scale(1)
+        z_make(2)
+        z_turn(2)
+        z_copy(0)
+        un_quantize(0)
+        z_make(3)
+        z_turn(3)
+        z_copy(1)
+        zi_interleave(768, 256, False)
+        zi_interleave(0, 256)
+        zi_interleave(256, 256)
+        z_quantize(0)
+        zi_quantize(0, 512)
+        zi_interleave(512, 256)
+        w_copy(2)
+        w_copy(3)
+        z_quantize(1)
+        zi_quantize(512, 512)
+        z_copy(2)
+        z_copy(3)
+        column_constants()
+        signed_sine()
+        w_quantize(0, 1)
+        z_quantize(2)
+        z_quantize(3)
+
+        plan = {}
+
+        def stream(first, pace, jobs):
+            for k, job in enumerate(jobs):
+                at = int(first + pace * k)
+                for s, step in enumerate(job):
+                    plan.setdefault(at + s, []).append(step)
+
+        def a_job(a, h):
+            def finish():
+                a_mul(a, h)
+                a_add(a, h)
+                a_store(a, h)
+            return [lambda: a_mm(a, h), finish]
+
+        def w_job(b):
+            def finish():
+                if b % 2 == 1:
+                    w_quantize(b // 4, b % 4 // 2)
+            if b in (99, 99):
+                return [lambda: w_direct(b), lambda: None, finish]
+            return [lambda: w_weave(b), lambda: w_copy(b), finish]
+
+        def t_job(b, j):
+            def finish():
+                t_copy(b, j)
+                if j % 4 == 3:
+                    t_store(b, j // 4)
+            return [lambda: t_mm(b, j), lambda: t_affine(b, j), lambda: t_turn(b, j), finish]
+
+        def u_job(b, hp):
+            def finish():
+                if hp == 1:
+                    un_quantize(b)
+            return [lambda: un_turn(b, hp), lambda: un_copy(b, hp), finish]
+
+        def k_job(tp, n):
+            def scale():
+                kv_scale(tp, 0, n)
+                if n == 1:
+                    k_cos(tp)
+            def sin():
+                if n == 1:
+                    k_sin(tp, 0, tp not in (9, 9))
+                    k_sin(tp, 1, tp not in (9, 9))
+            def nothing():
+                return None
+            def finish():
+                if n == 1:
+                    k_add(tp, tp not in (9, 9))
+                    k_store(tp)
+            return [lambda: kv_mm(tp, 0, n), scale, sin] + [nothing] * 1 + [finish]
+
+        def v_job(tp, n):
+            def scale():
+                if tp in (3, 9):
+                    v_tau(tp, n)
+                    v_bias(tp, n)
+                else:
+                    kv_scale(tp, 1, n)
+                if n == 1:
+                    v_store(tp)
+            return [lambda: kv_mm(tp, 1, n), scale]
+
+        by_turn = [(b, jh) for b, jh in ((1, 0), (1, 1), (3, 0), (3, 1))]
+        order = [(a, h) for b in (0, 2, 1, 3) for h in range(2) if (b, h) not in by_turn for a in range(4 * b, 4 * b + 4)]
+        stream(3.5, 1.045, [a_job(a, h) for a, h in order])
+        stream(1.5, 0.923, [w_job(b) for b in range(4, 16)])
+        stream(2.5, 1.607, [u_job(b, hp) for b in range(1, 4) for hp in range(2)])
+        stream(10.5, 1.118, [t_job(b, j) for b, jh in by_turn for j in range(4 * jh, 4 * jh + 4)])
+        stream(13.5, 2.055, [k_job(tp, n) for tp in range(4) for n in range(2)])
+        stream(15.5, 7.949, [v_job(tp, n) for tp in range(4) for n in range(2)])
+        for r in range(max(plan) + 1):
+            for step in plan.get(r, []):
+                step()

@@ -45,7 +45,7 @@ def tile_cache_pool_upproject_f6_kernel(
             return work.tile(shape, dtype, tag="s8", name=label, bufs=5, align_bytes=64)
 
         def small(shape, dtype, label):
-            return work.tile(shape, dtype, tag="s4", name=label, bufs=7, align_bytes=64)
+            return work.tile(shape, dtype, tag="s4", name=label, bufs=6, align_bytes=64)
 
         def loaded(shape, label):
             return work.tile(shape, BF16, tag="ld8", name=label, bufs=6, align_bytes=64)
@@ -110,24 +110,56 @@ def tile_cache_pool_upproject_f6_kernel(
         nc.gpsimd.dma_start(out=ss_b[:], in_=slot_scale.rearrange("(m t) -> m t", t=4))
         tau_b = keep.tile([P, 4], BF16, name="tau_b")
         nc.gpsimd.dma_start(out=tau_b[:], in_=tau.rearrange("(m t) -> m t", t=4))
-        cos_b = keep.tile([P, 4, HALF], BF16, name="cos_b")
-        nc.gpsimd.dma_start(out=cos_b[:], in_=cos_t.rearrange("(m t) d -> m t d", t=4))
-        sin_b = keep.tile([P, 4, HALF], BF16, name="sin_b")
-        nc.gpsimd.dma_start(out=sin_b[:], in_=sin_t.rearrange("(m t) d -> m t d", t=4))
+        cs_b = keep.tile([P, 4, 2, HALF], BF16, name="cs_b")
+        nc.gpsimd.dma_start(out=cs_b[:, :, 0, :], in_=cos_t.rearrange("(m t) d -> m t d", t=4))
+        nc.gpsimd.dma_start(out=cs_b[:, :, 1, :], in_=sin_t.rearrange("(m t) d -> m t d", t=4))
         cols = keep.tile([P, 16], F32, name="cols")
-        ssin = keep.tile([P, 4, 2, HALF], BF16, name="ssin")
+        tau_f = keep.tile([P, 4], F32, name="tau_f")
+        ctau = keep.tile([P, 4, HALF], F32, name="ctau")
+        stau = keep.tile([P, 4, 2, HALF], F32, name="stau")
+        cs_l = keep.tile([P, 4, P], BF16, name="cs_l")
+        rot_b = keep.tile([P, 8, 2, HALF], BF16, name="rot_b")
+        mask = keep.tile([P, 2, HALF], BF16, name="mask")
 
         def column_constants():
             turned = bank([P, P], "turned", BF16)
             nc.tensor.transpose(turned[:], rows[:], ident16[:])
             nc.vector.tensor_copy(out=cols[:], in_=turned[:, 0:16])
 
-        tau_f = keep.tile([P, 4], F32, name="tau_f")
+        def early_masks():
+            nc.vector.tensor_tensor(out=mask[:, 0, :], in0=ident16[:, 0:HALF], in1=ident16[:, HALF:P], op=ALU.add)
+            nc.vector.tensor_scalar(out=mask[:, 1, :], in0=mask[:, 0, :], scalar1=-1.0, scalar2=None, op0=ALU.mult)
 
-        def signed_sine():
+        def tau_tables():
             nc.vector.tensor_copy(out=tau_f[:], in_=tau_b[:])
-            nc.vector.tensor_scalar(out=ssin[:, :, 0, :], in0=sin_b[:], scalar1=-1.0, scalar2=None, op0=ALU.mult)
-            nc.vector.tensor_copy(out=ssin[:, :, 1, :], in_=sin_b[:])
+            by_slot = tau_f[:].unsqueeze(2).to_broadcast([P, 4, HALF])
+            nc.vector.tensor_tensor(out=ctau[:], in0=cs_b[:, :, 0, :], in1=by_slot, op=ALU.mult)
+            nc.vector.tensor_tensor(out=stau[:, :, 1, :], in0=cs_b[:, :, 1, :], in1=by_slot, op=ALU.mult)
+            nc.vector.tensor_scalar(out=stau[:, :, 0, :], in0=stau[:, :, 1, :], scalar1=-1.0, scalar2=None, op0=ALU.mult)
+
+        turned_cs = {}
+
+        def cs_turn():
+            cs_t = bank([P, 4, P], "cs_t", BF16)
+            for tp in range(4):
+                nc.tensor.transpose(cs_t[:, tp, :], cs_b[:, tp, :, :].rearrange("p s d -> p (s d)"), ident16[:])
+            turned_cs[0] = cs_t
+
+        def cs_copy():
+            nc.scalar.copy(out=cs_l[:], in_=turned_cs[0][:])
+
+        def rot_tables():
+            b_v = bup_b[:, 0:E].rearrange("p (h s d) -> p h s d", s=2, d=HALF)
+            lo, hi = slice(0, HALF), slice(HALF, P)
+            nc.vector.tensor_tensor(
+                out=rot_b[lo].rearrange("p h s d -> p (h s) d"), in0=bup_b[lo, 0:E].rearrange("p (g d) -> p g d", d=HALF),
+                in1=mask[lo, 0, :].unsqueeze(1).to_broadcast([HALF, 16, HALF]), op=ALU.mult,
+            )
+            for s in range(2):
+                nc.vector.tensor_tensor(
+                    out=rot_b[hi, :, s, :], in0=b_v[hi, :, 1 - s, :],
+                    in1=mask[hi, 1 - s, :].unsqueeze(1).to_broadcast([HALF, 8, HALF]), op=ALU.mult,
+                )
 
         def interleave(engine_copy, dst, src):
             engine_copy(
@@ -162,8 +194,8 @@ def tile_cache_pool_upproject_f6_kernel(
 
         def x_quantize(g, h):
             if g not in xq:
-                xq_g = work.tile([P, 1024], U32, tag="codes", name="xq", bufs=6, align_bytes=64)
-                xs_g = work.tile([P, 1024], U8, tag="scales", name="xs", bufs=6, align_bytes=64)
+                xq_g = work.tile([P, 1024], U32, tag="codes", name="xq", bufs=5, align_bytes=64)
+                xs_g = work.tile([P, 1024], U8, tag="scales", name="xs", bufs=5, align_bytes=64)
                 xq[g], xs[g] = xq_g, xs_g
             c = span(512 * h, 512)
             quantize(xq[g][:, c], xs[g][:, c], xi[g][:, c, :].rearrange("p c j -> p (c j)"))
@@ -330,8 +362,8 @@ def tile_cache_pool_upproject_f6_kernel(
 
         def w_quantize(q, h):
             if q not in wq:
-                wq_q = work.tile([P, 1024], U32, tag="codes", name="wq", bufs=6, align_bytes=64)
-                ws_q = work.tile([P, 1024], U8, tag="scales", name="ws", bufs=6, align_bytes=64)
+                wq_q = work.tile([P, 1024], U32, tag="codes", name="wq", bufs=5, align_bytes=64)
+                ws_q = work.tile([P, 1024], U8, tag="scales", name="ws", bufs=5, align_bytes=64)
                 wq[q], ws[q] = wq_q, ws_q
             c = span(512 * h, 512)
             quantize(wq[q][:, c], ws[q][:, c], wi[q][:, c, :].rearrange("p c j -> p (c j)"))
@@ -349,7 +381,7 @@ def tile_cache_pool_upproject_f6_kernel(
             )
 
         def a_mul(a, h):
-            ro_a = work.tile([P, 512], F32, tag="s2", name="ro", bufs=8)
+            ro_a = work.tile([P, 512], F32, tag="s2", name="ro", bufs=10)
             ro[a, h] = ro_a
             nc.vector.tensor_tensor(out=ro_a[:], in0=pa[a, h][:], in1=rest_b[:, span(512 * h, 512)], op=ALU.mult)
 
@@ -371,7 +403,7 @@ def tile_cache_pool_upproject_f6_kernel(
             )
 
         def t_affine(b, j):
-            r_t = work.tile([P, 512], F32, tag="s2", name="rt_s", bufs=8)
+            r_t = work.tile([P, 512], F32, tag="s2", name="rt_s", bufs=10)
             nc.scalar.activation(out=r_t[:], in_=pt[b, j][:], func=ACT.Identity, scale=cols[:, j : j + 1], bias=cols[:, 8 + j : 9 + j])
             rt_s[b, j] = r_t
 
@@ -394,7 +426,7 @@ def tile_cache_pool_upproject_f6_kernel(
 
         keys_view = keys.rearrange("(m t) e -> m t e", t=4)
         values_view = values.rearrange("(m t) e -> m t e", t=4)
-        pk, kv, m1, m2 = {}, {}, {}, {}
+        pk, kv, m1, m2, pbias, k_o = {}, {}, {}, {}, {}, {}
 
         def kv_mm(tp, h, n):
             pk_t = bank([P, 512], "pk")
@@ -427,30 +459,41 @@ def tile_cache_pool_upproject_f6_kernel(
             c = span(512 * n, 512)
             nc.gpsimd.tensor_tensor(out=kv[tp, 1][:, c], in0=kv[tp, 1][:, c], in1=bup_b[:, span(1024 + 512 * n, 512)], op=ALU.add)
 
-        def k_cos(tp, vector=False):
-            m1_t = small([P, 1024], F32, "m1")
-            m1[tp] = m1_t
-            (nc.vector if vector else nc.gpsimd).tensor_tensor(
-                out=m1_t[:].rearrange("p (h d) -> p h d", d=HALF), in0=kv[tp, 0][:].rearrange("p (h d) -> p h d", d=HALF),
-                in1=cos_b[:, tp, :].unsqueeze(1).to_broadcast([P, 16, HALF]), op=ALU.mult,
+        def kb_mm(tp, n):
+            pb_t = bank([P, 512], "pb")
+            pbias[tp, n] = pb_t
+            nc.tensor.matmul(
+                out=pb_t[:], lhsT=cs_l[:, tp, :], rhs=rot_b[:].rearrange("p h s d -> p (h s d)")[:, span(512 * n, 512)],
+                start=True, stop=True,
             )
 
-        def k_sin(tp, s, vector=True):
-            if s == 0:
-                m2_t = small([P, 1024], F32, "m2")
-                m2[tp] = m2_t
-            kh = kv[tp, 0][:].rearrange("p (h s d) -> p h s d", s=2, d=HALF)
-            mh = m2[tp][:].rearrange("p (h s d) -> p h s d", s=2, d=HALF)
-            (nc.vector if vector else nc.gpsimd).tensor_tensor(
-                out=mh[:, :, s, :], in0=kh[:, :, 1 - s, :],
-                in1=ssin[:, tp, s, :].unsqueeze(1).to_broadcast([P, 8, HALF]), op=ALU.mult,
+        def k_parts(tp, n):
+            m1_t = work.tile([P, 512], F32, tag="s2", name="m1", bufs=10)
+            m2_t = work.tile([P, 512], F32, tag="s2", name="m2", bufs=10)
+            m1[tp, n], m2[tp, n] = m1_t, m2_t
+            nc.vector.tensor_tensor(
+                out=m1_t[:].rearrange("p (h d) -> p h d", d=HALF), in0=pk[tp, 0, n][:].rearrange("p (h d) -> p h d", d=HALF),
+                in1=ctau[:, tp, :].unsqueeze(1).to_broadcast([P, 8, HALF]), op=ALU.mult,
             )
+            kh = pk[tp, 0, n][:].rearrange("p (h s d) -> p h s d", s=2, d=HALF)
+            mh = m2_t[:].rearrange("p (h s d) -> p h s d", s=2, d=HALF)
+            for s in range(2):
+                nc.vector.tensor_tensor(
+                    out=mh[:, :, s, :], in0=kh[:, :, 1 - s, :],
+                    in1=stau[:, tp, s, :].unsqueeze(1).to_broadcast([P, 4, HALF]), op=ALU.mult,
+                )
 
-        def k_add(tp, vector=True):
-            (nc.vector if vector else nc.gpsimd).tensor_tensor(out=m1[tp][:], in0=m1[tp][:], in1=m2[tp][:], op=ALU.add)
+        def k_sum(tp, n):
+            nc.gpsimd.tensor_tensor(out=m1[tp, n][:], in0=m1[tp, n][:], in1=m2[tp, n][:], op=ALU.add)
+
+        def k_bias(tp, n):
+            if tp not in k_o:
+                k_t = small([P, 1024], F32, "k_o")
+                k_o[tp] = k_t
+            nc.vector.tensor_tensor(out=k_o[tp][:, span(512 * n, 512)], in0=pbias[tp, n][:], in1=m1[tp, n][:], op=ALU.add)
 
         def k_store(tp):
-            nc.sync.dma_start(out=keys_view[:, tp, :], in_=m1[tp][:])
+            nc.sync.dma_start(out=keys_view[:, tp, :], in_=k_o[tp][:])
 
         def v_store(tp):
             nc.sync.dma_start(out=values_view[:, tp, :], in_=kv[tp, 1][:])
@@ -462,6 +505,7 @@ def tile_cache_pool_upproject_f6_kernel(
             pool_turn(0, hp)
         for hp in range(2):
             pool_copy(0, hp)
+        early_masks()
         for g in range(4):
             nxt = g + 1
             if nxt < 4:
@@ -539,7 +583,9 @@ def tile_cache_pool_upproject_f6_kernel(
         z_copy(2)
         z_copy(3)
         column_constants()
-        signed_sine()
+        tau_tables()
+        cs_turn()
+        cs_copy()
         w_quantize(0, 1)
         z_quantize(2)
         z_quantize(3)
@@ -552,19 +598,24 @@ def tile_cache_pool_upproject_f6_kernel(
                 for s, step in enumerate(job):
                     plan.setdefault(at + s, []).append(step)
 
-        def a_job(a, h):
+        def a_job(a, h, vector):
             def finish():
                 a_mul(a, h)
-                a_add(a, h)
-                a_store(a, h)
-            return [lambda: a_mm(a, h), finish]
+                if not vector:
+                    a_add(a, h)
+                    a_store(a, h)
+            def late():
+                if vector:
+                    a_add(a, h, True)
+                    a_store(a, h)
+            return [lambda: a_mm(a, h), finish, late]
 
         def w_job(b):
             def finish():
                 if b % 2 == 1:
                     w_quantize(b // 4, b % 4 // 2)
-            if b in (99, 99):
-                return [lambda: w_direct(b), lambda: None, finish]
+            if b in (13, 99):
+                return [lambda: w_direct(b, True), lambda: None, finish]
             return [lambda: w_weave(b), lambda: w_copy(b), finish]
 
         def t_job(b, j):
@@ -581,25 +632,18 @@ def tile_cache_pool_upproject_f6_kernel(
             return [lambda: un_turn(b, hp), lambda: un_copy(b, hp), finish]
 
         def k_job(tp, n):
-            def scale():
-                kv_scale(tp, 0, n)
-                if n == 1:
-                    k_cos(tp)
-            def sin():
-                if n == 1:
-                    k_sin(tp, 0, tp not in (9, 9))
-                    k_sin(tp, 1, tp not in (9, 9))
-            def nothing():
-                return None
+            def parts():
+                k_parts(tp, n)
+                k_sum(tp, n)
             def finish():
+                k_bias(tp, n)
                 if n == 1:
-                    k_add(tp, tp not in (9, 9))
                     k_store(tp)
-            return [lambda: kv_mm(tp, 0, n), scale, sin] + [nothing] * 1 + [finish]
+            return [lambda: kv_mm(tp, 0, n), parts] + [lambda: None] * 4 + [lambda: kb_mm(tp, n), finish]
 
         def v_job(tp, n):
             def scale():
-                if tp in (3, 9):
+                if (tp, n) in ((9, 9), (9, 9)):
                     v_tau(tp, n)
                     v_bias(tp, n)
                 else:
@@ -608,14 +652,16 @@ def tile_cache_pool_upproject_f6_kernel(
                     v_store(tp)
             return [lambda: kv_mm(tp, 1, n), scale]
 
-        by_turn = [(b, jh) for b, jh in ((1, 0), (1, 1), (3, 0), (3, 1))]
-        order = [(a, h) for b in (0, 2, 1, 3) for h in range(2) if (b, h) not in by_turn for a in range(4 * b, 4 * b + 4)]
-        stream(3.5, 1.045, [a_job(a, h) for a, h in order])
-        stream(1.5, 0.923, [w_job(b) for b in range(4, 16)])
-        stream(2.5, 1.607, [u_job(b, hp) for b in range(1, 4) for hp in range(2)])
-        stream(10.5, 1.118, [t_job(b, j) for b, jh in by_turn for j in range(4 * jh, 4 * jh + 4)])
-        stream(13.5, 2.055, [k_job(tp, n) for tp in range(4) for n in range(2)])
-        stream(15.5, 7.949, [v_job(tp, n) for tp in range(4) for n in range(2)])
+        by_turn = [(b, jh) for b, jh in ((1, 0), (1, 1), (3, 0), (3, 1), (2, 1))]
+        order = [(a, h) for b in (0, 1, 2, 3) for h in range(2) if (b, h) not in by_turn for a in range(4 * b, 4 * b + 4)]
+        stream(3.5, 2.794, [a_job(a, h, True) for a, h in order[:5]])
+        stream(14.5, 1.389, [a_job(a, h, False) for a, h in order[5:]])
+        stream(0, 1.714, [w_job(b) for b in range(4, 16)])
+        stream(0, 2.523, [u_job(b, hp) for b in range(1, 4) for hp in range(2)])
+        stream(11, 1, [[rot_tables]])
+        stream(8, 1.116, [t_job(b, j) for b, jh in by_turn for j in range(4 * jh, 4 * jh + 4)])
+        stream(15, 2.643, [k_job(tp, n) for tp in range(4) for n in range(2)])
+        stream(19, 1.523, [v_job(tp, n) for tp in range(4) for n in range(2)])
         for r in range(max(plan) + 1):
             for step in plan.get(r, []):
                 step()

@@ -54,66 +54,78 @@ def tile_cache_pool_upproject_f6_kernel(
         nc.scalar.dma_start(out=xsc[:], in_=x_scale.rearrange("(g p t) o -> p g (t o)", p=P, t=4))
         x_view = x_bytes.rearrange("(g p t) d -> g p t d", p=P, t=4)
         pool_view = pool.rearrange("(m t) k -> m t k", t=4)
-        xb = {}
+        rows = keep.tile([P, P], BF16, name="rows")
+        nc.vector.memset(rows[:], 0.0)
+        xb = []
         pr = []
-        for g in range(4):
-            for th in range(2):
-                xb_g = keep.tile([P, 2, D], U8, name="xb%d%d" % (g, th), align_bytes=64)
-                nc.sync.dma_start(out=xb_g[:], in_=x_view[g][:, span(2 * th, 2), :])
-                xb[g, th] = xb_g
-            if g % 2 == 0:
-                pr_g = loaded([P, 4, 1024], "pr")
-                pr.append(pr_g)
-            nc.sync.dma_start(out=pr[g // 2][:, :, span(512 * (g % 2), 512)], in_=pool_view[:, :, span(512 * g, 512)])
-        w_view = w_up.rearrange("(g p t) n -> g p t n", p=P, t=4)
+        un = []
         wr = {}
+        ss_b = keep.tile([P, 4], BF16, name="ss_b")
+        tau_b = keep.tile([P, 4], BF16, name="tau_b")
+        cs_b = keep.tile([P, 4, 2, HALF], BF16, name="cs_b")
+        emb = keep.tile([P, 4, D], BF16, name="emb")
+        un_view = unpool.rearrange("(p a) s -> p a s", a=16)
+        w_view = w_up.rearrange("(g p t) n -> g p t n", p=P, t=4)
+
+        def load_x(g):
+            xb_g = keep.tile([P, 4, D], U8, name="xb%d" % g, align_bytes=64)
+            for part in range(2 if g == 0 else 1):
+                n = span(2 * part, 2) if g == 0 else span(0, 4)
+                nc.sync.dma_start(out=xb_g[:, n, :], in_=x_view[g][:, n, :])
+            xb.append(xb_g)
+
+        def load_pool(i):
+            pr_i = loaded([P, 4, 1024], "pr")
+            nc.sync.dma_start(out=pr_i[:], in_=pool_view[:, :, span(1024 * i, 1024)])
+            pr.append(pr_i)
+
+        def load_un(i):
+            un_i = loaded([P, 8, S], "un")
+            nc.sync.dma_start(out=un_i[:], in_=un_view[:, span(8 * i, 8), :])
+            un.append(un_i)
 
         def load_w(q):
             w_q = loaded([P, 4, 1024], "wr")
             nc.sync.dma_start(out=w_q[:], in_=w_view[q % 2][:, :, span(1024 * (q // 2), 1024)])
             wr[q] = w_q
 
+        load_x(0)
+        load_x(1)
+        load_pool(0)
+        at = 0
+        for vec, n in ((gain, 8), (restore, 8), (b_rec, 8), (b_up, 16)):
+            nc.sync.dma_start(out=rows[at : at + n, :], in_=vec.rearrange("(j p) -> j p", p=P))
+            at += n
+        load_x(2)
+        load_x(3)
+        load_pool(1)
+        nc.sync.dma_start(out=ss_b[:], in_=slot_scale.rearrange("(m t) -> m t", t=4))
+        nc.sync.dma_start(out=tau_b[:], in_=tau.rearrange("(m t) -> m t", t=4))
         load_w(0)
-        emb = keep.tile([P, 4, D], BF16, name="emb")
         nc.sync.dma_start(out=emb[:], in_=slot_emb.rearrange("(m t) d -> m t d", t=4))
-        gain_b = keep.tile([P, D], BF16, name="gain_b")
-        nc.sync.dma_start(out=gain_b[:], in_=gain.partition_broadcast(P))
+        load_un(0)
+        load_un(1)
         load_w(1)
-        un_view = unpool.rearrange("(p a) s -> p a s", a=16)
-        un = []
-        for i in range(2):
-            un_i = loaded([P, 8, S], "un")
-            nc.sync.dma_start(out=un_i[:], in_=un_view[:, span(8 * i, 8), :])
-            un.append(un_i)
-        rest_b = keep.tile([P, D], BF16, name="rest_b")
-        nc.sync.dma_start(out=rest_b[:], in_=restore.partition_broadcast(P))
-        brec_b = keep.tile([P, D], BF16, name="brec_b")
-        nc.sync.dma_start(out=brec_b[:], in_=b_rec.partition_broadcast(P))
+        nc.sync.dma_start(out=cs_b[:, :, 0, :], in_=cos_t.rearrange("(m t) d -> m t d", t=4))
+        nc.sync.dma_start(out=cs_b[:, :, 1, :], in_=sin_t.rearrange("(m t) d -> m t d", t=4))
         load_w(2)
         load_w(3)
-        bup_b = keep.tile([P, 2 * E], BF16, name="bup_b")
-        nc.sync.dma_start(out=bup_b[:], in_=b_up.partition_broadcast(P))
 
         one = keep.tile([P, 1], F32, name="one")
         nc.vector.memset(one[:], 1.0)
-        rows = keep.tile([P, P], BF16, name="rows")
-        nc.vector.memset(rows[:], 0.0)
         warm = keep.tile([P, 1], F32, name="warm")
         nc.scalar.activation(out=warm[:], in_=one[:], func=ACT.Sqrt)
         ident = keep.tile([P, P], F32, name="ident")
         make_identity(nc, ident[:])
         ident16 = keep.tile([P, P], BF16, name="ident16")
         make_identity(nc, ident16[:])
-        nc.gpsimd.dma_start(out=rows[0:8, :], in_=restore.rearrange("(j p) -> j p", p=P))
-        nc.gpsimd.dma_start(out=rows[8:16, :], in_=b_rec.rearrange("(j p) -> j p", p=P))
-        ss_b = keep.tile([P, 4], BF16, name="ss_b")
-        nc.gpsimd.dma_start(out=ss_b[:], in_=slot_scale.rearrange("(m t) -> m t", t=4))
-        tau_b = keep.tile([P, 4], BF16, name="tau_b")
-        nc.gpsimd.dma_start(out=tau_b[:], in_=tau.rearrange("(m t) -> m t", t=4))
-        cs_b = keep.tile([P, 4, 2, HALF], BF16, name="cs_b")
-        nc.gpsimd.dma_start(out=cs_b[:, :, 0, :], in_=cos_t.rearrange("(m t) d -> m t d", t=4))
-        nc.gpsimd.dma_start(out=cs_b[:, :, 1, :], in_=sin_t.rearrange("(m t) d -> m t d", t=4))
+        cols16 = keep.tile([P, 40], BF16, name="cols16")
         cols = keep.tile([P, 16], F32, name="cols")
+        vecs = keep.tile([P, 5, D], BF16, name="vecs")
+        gain_b, rest_b, brec_b = vecs[:, 0, :], vecs[:, 1, :], vecs[:, 2, :]
+        bup_b = vecs[:, 3:5, :].rearrange("p a d -> p (a d)")
+        spread_p = {}
+
         tau_f = keep.tile([P, 4], F32, name="tau_f")
         ctau = keep.tile([P, 4, HALF], F32, name="ctau")
         stau = keep.tile([P, 4, 2, HALF], F32, name="stau")
@@ -121,10 +133,24 @@ def tile_cache_pool_upproject_f6_kernel(
         rot_b = keep.tile([P, 8, 2, HALF], BF16, name="rot_b")
         mask = keep.tile([P, 2, HALF], BF16, name="mask")
 
-        def column_constants():
+        def turn_rows():
             turned = bank([P, P], "turned", BF16)
             nc.tensor.transpose(turned[:], rows[:], ident16[:])
-            nc.vector.tensor_copy(out=cols[:], in_=turned[:, 0:16])
+            spread_p[-1] = turned
+
+        def turn_copy():
+            nc.vector.tensor_copy(out=cols16[:], in_=spread_p[-1][:, 0:40])
+            nc.vector.tensor_copy(out=cols[:], in_=cols16[:, 8:24])
+
+        def spread(i):
+            sp = bank([P, 8, P], "sp", BF16)
+            spread_p[i] = sp
+            for j in range(8):
+                nc.tensor.transpose(sp[:, j, :], cols16[:, 8 * i + j : 8 * i + j + 1].to_broadcast([P, P]), ident16[:])
+
+        def spread_copy(i, vector=False):
+            fn = nc.vector.tensor_copy if vector else nc.scalar.copy
+            fn(out=vecs[:, i, :], in_=spread_p[i][:].rearrange("p j m -> p (j m)"))
 
         def early_masks():
             nc.vector.tensor_tensor(out=mask[:, 0, :], in0=ident16[:, 0:HALF], in1=ident16[:, HALF:P], op=ALU.add)
@@ -178,7 +204,7 @@ def tile_cache_pool_upproject_f6_kernel(
                 xw_g = big([P, 4, D], BF16, "xw")
                 xw[g] = xw_g
             c = span(at, width)
-            src = xb[g, t // 2][:, t % 2, c].bitcast(FP8)
+            src = xb[g][:, t, c].bitcast(FP8)
             scale = xsc[:, g, t : t + 1]
             if vector:
                 nc.vector.tensor_scalar(out=xw[g][:, t, c], in0=src, scalar1=scale, scalar2=None, op0=ALU.mult)
@@ -269,7 +295,7 @@ def tile_cache_pool_upproject_f6_kernel(
             nc.vector.tensor_tensor(out=rs[:, n], in0=rr[:, n], in1=ss_b[:, n], op=ALU.mult)
 
         def z_make(tp):
-            nc.vector.scalar_tensor_tensor(out=zb[:, tp, :], in0=c_f[tp][:], scalar=rs[:, tp : tp + 1], in1=gain_b[:], op0=ALU.mult, op1=ALU.mult)
+            nc.vector.scalar_tensor_tensor(out=zb[:, tp, :], in0=c_f[tp][:], scalar=rs[:, tp : tp + 1], in1=gain_b, op0=ALU.mult, op1=ALU.mult)
 
         def z_turn(tp):
             zw = words(zb[:, tp, :])
@@ -501,102 +527,119 @@ def tile_cache_pool_upproject_f6_kernel(
         for h in range(2):
             for t in range(4):
                 x_widen(0, t, t % 2 == 1, 512 * h, 512)
+        early_masks()
+        by_vector = (0, 1, 0, 1)
+        counts = (0, 0, 2, 2)
+        woven = [list(range(sum(counts[:g]), sum(counts[: g + 1]))) for g in range(4)]
+        done = sum(counts)
+        spreads = ((), (), (), (0, 1))
         for hp in range(2):
             pool_turn(0, hp)
-        for hp in range(2):
-            pool_copy(0, hp)
-        early_masks()
         for g in range(4):
             nxt = g + 1
             if nxt < 4:
+                for t in range(4 - by_vector[nxt]):
+                    x_widen(nxt, t, False)
+            for hp in range(2):
+                pool_copy(g, hp)
+            if g == 1:
+                turn_rows()
+            if nxt < 4:
                 for hp in range(2):
                     pool_turn(nxt, hp)
-                for t in range(3 if nxt in (1, 3) else 4):
-                    x_widen(nxt, t, False)
+            for i in spreads[g]:
+                spread(i)
+            for b in woven[g]:
+                w_weave(b)
             x_interleave(g, 0, 512)
-            pool_quantize(g)
+            if g == 1:
+                turn_copy()
             if g < 3:
                 x_interleave(g, 512, 512)
             else:
                 x_interleave(g, 768, 256, False)
                 x_interleave(g, 512, 256)
             x_quantize(g, 0)
-            if nxt in (1, 3):
-                x_widen(nxt, 3, True)
-            x_quantize(g, 1)
             if nxt < 4:
-                for hp in range(2):
-                    pool_copy(nxt, hp)
-            if g == 3:
-                for k in range(3):
-                    for h in range(2):
-                        pooled(3, k, h)
-            for tp in range(4 if g == 3 else 3):
+                for t in range(4 - by_vector[nxt], 4):
+                    x_widen(nxt, t, True)
+            x_quantize(g, 1)
+            pool_quantize(g)
+            for i in spreads[g]:
+                spread_copy(i, i in (0, 9))
+            for tp in range(2):
                 for h in range(2):
                     pooled(tp, g, h)
-            if 1 <= g < 3:
-                w_weave(g - 1)
-                w_copy(g - 1)
+            for b in woven[g]:
+                w_copy(b)
 
-        for tp in range(4):
+        for tp in range(2, 4):
+            for k in range(4):
+                for h in range(2):
+                    pooled(tp, k, h)
+        for tp in range(3):
             c_add(tp, 0)
             c_add(tp, 1)
-            if tp == 0:
-                un_turn(0, 0)
-                un_turn(0, 1)
-            if tp == 1:
-                w_weave(2)
-                w_weave(3)
-        for tp in range(3):
             c_square(tp)
+        if done > 1:
+            w_quantize(0, 0)
         c_mean(0)
-        w_quantize(0, 0)
         c_root(0)
+        un_turn(0, 0)
+        un_turn(0, 1)
+        c_add(3, 0)
+        c_add(3, 1)
         c_square(3)
         c_scale(0)
         z_make(0)
         z_turn(0)
         un_copy(0, 0)
-        c_mean(1)
-        c_root(1)
         z_make(1)
         z_turn(1)
         un_copy(0, 1)
+        c_mean(1)
+        c_root(1)
+        un_quantize(0)
+        un_turn(1, 0)
+        un_turn(1, 1)
         c_scale(1)
+        z_copy(0)
+        z_copy(1)
         z_make(2)
         z_turn(2)
-        z_copy(0)
-        un_quantize(0)
+        un_copy(1, 0)
+        un_copy(1, 1)
+        for i in range(1, done // 2):
+            w_quantize(i // 2, i % 2)
         z_make(3)
         z_turn(3)
-        z_copy(1)
         zi_interleave(768, 256, False)
         zi_interleave(0, 256)
         zi_interleave(256, 256)
         z_quantize(0)
         zi_quantize(0, 512)
         zi_interleave(512, 256)
-        w_copy(2)
-        w_copy(3)
-        z_quantize(1)
-        zi_quantize(512, 512)
         z_copy(2)
         z_copy(3)
-        column_constants()
+        z_quantize(1)
+        zi_quantize(512, 512)
+        for i in (2, 3, 4):
+            spread(i)
+            spread_copy(i, i in (0, 9))
         tau_tables()
         cs_turn()
         cs_copy()
-        w_quantize(0, 1)
+        un_quantize(1)
         z_quantize(2)
         z_quantize(3)
 
         plan = {}
 
-        def stream(first, pace, jobs):
+        def stream(first, pace, jobs, turn=-1):
             for k, job in enumerate(jobs):
                 at = int(first + pace * k)
                 for s, step in enumerate(job):
-                    plan.setdefault(at + s, []).append(step)
+                    plan.setdefault((at + s, s != turn), []).append(step)
 
         def a_job(a, h, vector):
             def finish():
@@ -618,12 +661,18 @@ def tile_cache_pool_upproject_f6_kernel(
                 return [lambda: w_direct(b, True), lambda: None, finish]
             return [lambda: w_weave(b), lambda: w_copy(b), finish]
 
-        def t_job(b, j):
+        def t_job(units):
+            def each(fn):
+                def run():
+                    for b, j in units:
+                        fn(b, j)
+                return run
             def finish():
-                t_copy(b, j)
-                if j % 4 == 3:
-                    t_store(b, j // 4)
-            return [lambda: t_mm(b, j), lambda: t_affine(b, j), lambda: t_turn(b, j), finish]
+                for b, j in units:
+                    t_copy(b, j, j % 8 in (7, 9))
+                    if j % 4 == 3:
+                        t_store(b, j // 4)
+            return [each(t_mm), each(t_affine), each(t_turn), finish]
 
         def u_job(b, hp):
             def finish():
@@ -639,7 +688,7 @@ def tile_cache_pool_upproject_f6_kernel(
                 k_bias(tp, n)
                 if n == 1:
                     k_store(tp)
-            return [lambda: kv_mm(tp, 0, n), parts] + [lambda: None] * 4 + [lambda: kb_mm(tp, n), finish]
+            return [lambda: kv_mm(tp, 0, n), parts] + [lambda: None] * 2 + [lambda: kb_mm(tp, n), finish]
 
         def v_job(tp, n):
             def scale():
@@ -652,16 +701,17 @@ def tile_cache_pool_upproject_f6_kernel(
                     v_store(tp)
             return [lambda: kv_mm(tp, 1, n), scale]
 
-        by_turn = [(b, jh) for b, jh in ((1, 0), (1, 1), (3, 0), (3, 1), (2, 1))]
-        order = [(a, h) for b in (0, 1, 2, 3) for h in range(2) if (b, h) not in by_turn for a in range(4 * b, 4 * b + 4)]
-        stream(3.5, 2.794, [a_job(a, h, True) for a, h in order[:5]])
-        stream(14.5, 1.389, [a_job(a, h, False) for a, h in order[5:]])
-        stream(0, 1.714, [w_job(b) for b in range(4, 16)])
-        stream(0, 2.523, [u_job(b, hp) for b in range(1, 4) for hp in range(2)])
-        stream(11, 1, [[rot_tables]])
-        stream(8, 1.116, [t_job(b, j) for b, jh in by_turn for j in range(4 * jh, 4 * jh + 4)])
-        stream(15, 2.643, [k_job(tp, n) for tp in range(4) for n in range(2)])
-        stream(19, 1.523, [v_job(tp, n) for tp in range(4) for n in range(2)])
-        for r in range(max(plan) + 1):
-            for step in plan.get(r, []):
+        by_turn = [(b, jh) for b, jh in ((1, 0), (1, 1), (2, 1), (3, 0), (3, 1))]
+        order = [(a, h) for b in (0, 2, 1, 3) for h in range(2) if (b, h) not in by_turn for a in range(4 * b, 4 * b + 4)]
+        stream(7.5, 0.622, [a_job(a, h, True) for a, h in order[:3]])
+        stream(12.5, 1.184, [a_job(a, h, False) for a, h in order[3:]])
+        stream(1, 1.272, [w_job(b) for b in range(done, 16)])
+        stream(0, 0.296, [u_job(b, hp) for b in range(2, 4) for hp in range(2)], 0)
+        stream(0, 1, [[rot_tables]])
+        units = [(b, j) for b, jh in by_turn for j in range(4 * jh, 4 * jh + 4)]
+        stream(8.5, 2.354, [t_job(units[i : i + 2]) for i in range(0, len(units), 2)], 2)
+        stream(18.5, 1.949, [k_job(tp, n) for tp in range(4) for n in range(2)])
+        stream(16, 0.989, [v_job(tp, n) for tp in range(4) for n in range(2)])
+        for key in sorted(plan):
+            for step in plan[key]:
                 step()

@@ -45,7 +45,7 @@ def tile_cache_pool_upproject_f6_kernel(
             return work.tile(shape, dtype, tag="s8", name=label, bufs=5, align_bytes=64)
 
         def small(shape, dtype, label):
-            return work.tile(shape, dtype, tag="s4", name=label, bufs=6, align_bytes=64)
+            return work.tile(shape, dtype, tag="s4", name=label, bufs=9, align_bytes=64)
 
         def loaded(shape, label):
             return work.tile(shape, BF16, tag="ld8", name=label, bufs=6, align_bytes=64)
@@ -62,7 +62,8 @@ def tile_cache_pool_upproject_f6_kernel(
         wr = {}
         ss_b = keep.tile([P, 4], BF16, name="ss_b")
         tau_b = keep.tile([P, 4], BF16, name="tau_b")
-        cs_b = keep.tile([P, 4, 2, HALF], BF16, name="cs_b")
+        cos_b = keep.tile([P, 4, HALF], BF16, name="cos_b")
+        sin_b = keep.tile([P, 4, HALF], BF16, name="sin_b")
         emb = keep.tile([P, 4, D], BF16, name="emb")
         un_view = unpool.rearrange("(p a) s -> p a s", a=16)
         w_view = w_up.rearrange("(g p t) n -> g p t n", p=P, t=4)
@@ -89,27 +90,29 @@ def tile_cache_pool_upproject_f6_kernel(
             nc.sync.dma_start(out=w_q[:], in_=w_view[q % 2][:, :, span(1024 * (q // 2), 1024)])
             wr[q] = w_q
 
+        gain_b = keep.tile([P, D], BF16, name="gain_b")
+        bup_b = keep.tile([P, 2 * E], BF16, name="bup_b")
         load_x(0)
         load_x(1)
         load_pool(0)
-        at = 0
-        for vec, n in ((gain, 8), (restore, 8), (b_rec, 8), (b_up, 16)):
-            nc.sync.dma_start(out=rows[at : at + n, :], in_=vec.rearrange("(j p) -> j p", p=P))
-            at += n
         load_x(2)
         load_x(3)
         load_pool(1)
         nc.sync.dma_start(out=ss_b[:], in_=slot_scale.rearrange("(m t) -> m t", t=4))
-        nc.sync.dma_start(out=tau_b[:], in_=tau.rearrange("(m t) -> m t", t=4))
-        load_w(0)
-        nc.sync.dma_start(out=emb[:], in_=slot_emb.rearrange("(m t) d -> m t d", t=4))
+        nc.sync.dma_start(out=rows[0:8, :], in_=restore.rearrange("(j p) -> j p", p=P))
+        nc.sync.dma_start(out=rows[8:16, :], in_=b_rec.rearrange("(j p) -> j p", p=P))
         load_un(0)
+        nc.sync.dma_start(out=emb[:], in_=slot_emb.rearrange("(m t) d -> m t d", t=4))
+        nc.sync.dma_start(out=gain_b[:], in_=gain.partition_broadcast(P))
+        load_w(0)
         load_un(1)
         load_w(1)
-        nc.sync.dma_start(out=cs_b[:, :, 0, :], in_=cos_t.rearrange("(m t) d -> m t d", t=4))
-        nc.sync.dma_start(out=cs_b[:, :, 1, :], in_=sin_t.rearrange("(m t) d -> m t d", t=4))
+        nc.sync.dma_start(out=tau_b[:], in_=tau.rearrange("(m t) -> m t", t=4))
+        nc.sync.dma_start(out=cos_b[:], in_=cos_t.rearrange("(m t) d -> m t d", t=4))
+        nc.sync.dma_start(out=sin_b[:], in_=sin_t.rearrange("(m t) d -> m t d", t=4))
         load_w(2)
         load_w(3)
+        nc.sync.dma_start(out=bup_b[:], in_=b_up.partition_broadcast(P))
 
         one = keep.tile([P, 1], F32, name="one")
         nc.vector.memset(one[:], 1.0)
@@ -119,73 +122,20 @@ def tile_cache_pool_upproject_f6_kernel(
         make_identity(nc, ident[:])
         ident16 = keep.tile([P, P], BF16, name="ident16")
         make_identity(nc, ident16[:])
-        cols16 = keep.tile([P, 40], BF16, name="cols16")
         cols = keep.tile([P, 16], F32, name="cols")
-        vecs = keep.tile([P, 5, D], BF16, name="vecs")
-        gain_b, rest_b, brec_b = vecs[:, 0, :], vecs[:, 1, :], vecs[:, 2, :]
-        bup_b = vecs[:, 3:5, :].rearrange("p a d -> p (a d)")
-        spread_p = {}
-
-        tau_f = keep.tile([P, 4], F32, name="tau_f")
-        ctau = keep.tile([P, 4, HALF], F32, name="ctau")
-        stau = keep.tile([P, 4, 2, HALF], F32, name="stau")
-        cs_l = keep.tile([P, 4, P], BF16, name="cs_l")
-        rot_b = keep.tile([P, 8, 2, HALF], BF16, name="rot_b")
-        mask = keep.tile([P, 2, HALF], BF16, name="mask")
+        ssin = keep.tile([P, 4, 2, HALF], BF16, name="ssin")
+        turned = {}
 
         def turn_rows():
-            turned = bank([P, P], "turned", BF16)
-            nc.tensor.transpose(turned[:], rows[:], ident16[:])
-            spread_p[-1] = turned
+            turned[0] = bank([P, P], "turned", BF16)
+            nc.tensor.transpose(turned[0][:], rows[:], ident16[:])
 
         def turn_copy():
-            nc.vector.tensor_copy(out=cols16[:], in_=spread_p[-1][:, 0:40])
-            nc.vector.tensor_copy(out=cols[:], in_=cols16[:, 8:24])
+            nc.vector.tensor_copy(out=cols[:], in_=turned[0][:, 0:16])
 
-        def spread(i):
-            sp = bank([P, 8, P], "sp", BF16)
-            spread_p[i] = sp
-            for j in range(8):
-                nc.tensor.transpose(sp[:, j, :], cols16[:, 8 * i + j : 8 * i + j + 1].to_broadcast([P, P]), ident16[:])
-
-        def spread_copy(i, vector=False):
-            fn = nc.vector.tensor_copy if vector else nc.scalar.copy
-            fn(out=vecs[:, i, :], in_=spread_p[i][:].rearrange("p j m -> p (j m)"))
-
-        def early_masks():
-            nc.vector.tensor_tensor(out=mask[:, 0, :], in0=ident16[:, 0:HALF], in1=ident16[:, HALF:P], op=ALU.add)
-            nc.vector.tensor_scalar(out=mask[:, 1, :], in0=mask[:, 0, :], scalar1=-1.0, scalar2=None, op0=ALU.mult)
-
-        def tau_tables():
-            nc.vector.tensor_copy(out=tau_f[:], in_=tau_b[:])
-            by_slot = tau_f[:].unsqueeze(2).to_broadcast([P, 4, HALF])
-            nc.vector.tensor_tensor(out=ctau[:], in0=cs_b[:, :, 0, :], in1=by_slot, op=ALU.mult)
-            nc.vector.tensor_tensor(out=stau[:, :, 1, :], in0=cs_b[:, :, 1, :], in1=by_slot, op=ALU.mult)
-            nc.vector.tensor_scalar(out=stau[:, :, 0, :], in0=stau[:, :, 1, :], scalar1=-1.0, scalar2=None, op0=ALU.mult)
-
-        turned_cs = {}
-
-        def cs_turn():
-            cs_t = bank([P, 4, P], "cs_t", BF16)
-            for tp in range(4):
-                nc.tensor.transpose(cs_t[:, tp, :], cs_b[:, tp, :, :].rearrange("p s d -> p (s d)"), ident16[:])
-            turned_cs[0] = cs_t
-
-        def cs_copy():
-            nc.scalar.copy(out=cs_l[:], in_=turned_cs[0][:])
-
-        def rot_tables():
-            b_v = bup_b[:, 0:E].rearrange("p (h s d) -> p h s d", s=2, d=HALF)
-            lo, hi = slice(0, HALF), slice(HALF, P)
-            nc.vector.tensor_tensor(
-                out=rot_b[lo].rearrange("p h s d -> p (h s) d"), in0=bup_b[lo, 0:E].rearrange("p (g d) -> p g d", d=HALF),
-                in1=mask[lo, 0, :].unsqueeze(1).to_broadcast([HALF, 16, HALF]), op=ALU.mult,
-            )
-            for s in range(2):
-                nc.vector.tensor_tensor(
-                    out=rot_b[hi, :, s, :], in0=b_v[hi, :, 1 - s, :],
-                    in1=mask[hi, 1 - s, :].unsqueeze(1).to_broadcast([HALF, 8, HALF]), op=ALU.mult,
-                )
+        def signed_sine():
+            nc.vector.tensor_scalar(out=ssin[:, :, 0, :], in0=sin_b[:], scalar1=-1.0, scalar2=None, op0=ALU.mult)
+            nc.vector.tensor_copy(out=ssin[:, :, 1, :], in_=sin_b[:])
 
         def interleave(engine_copy, dst, src):
             engine_copy(
@@ -358,28 +308,12 @@ def tile_cache_pool_upproject_f6_kernel(
             c = span(512 * b, 512)
             quantize(uq[:, c], us[:, c], ui[b][:].rearrange("p a m j -> p (a m j)"))
 
-        wp, wi, wq, ws = {}, {}, {}, {}
-
-        def w_weave(b):
-            q, c = b // 4, 256 * (b % 4)
-            wp_b = bank([P, 256, 4], "wp", BF16)
-            wp[b] = wp_b
-            for n in range(2):
-                nc.tensor.matmul(
-                    out=wp_b[:, span(128 * n, 128), :].rearrange("p c t -> p (c t)"), lhsT=ident16[:],
-                    rhs=wr[q][:, :, span(c + 128 * n, 128)].rearrange("p t c -> p c t"), start=True, stop=True,
-                )
+        wi, wq, ws = {}, {}, {}
 
         def w_tile(q):
             if q not in wi:
                 wi_q = big([P, 1024, 4], BF16, "wi")
                 wi[q] = wi_q
-
-        def w_copy(b, vector=False):
-            q = b // 4
-            w_tile(q)
-            fn = nc.vector.tensor_copy if vector else nc.scalar.copy
-            fn(out=wi[q][:, span(256 * (b % 4), 256), :], in_=wp[b][:])
 
         def w_direct(b, vector=True):
             q, c = b // 4, span(256 * (b % 4), 256)
@@ -395,28 +329,6 @@ def tile_cache_pool_upproject_f6_kernel(
             quantize(wq[q][:, c], ws[q][:, c], wi[q][:, c, :].rearrange("p c j -> p (c j)"))
 
         rec_view = rec.rearrange("(p a) d -> p a d", a=16)
-        pa, ro = {}, {}
-
-        def a_mm(a, h):
-            pa_t = bank([P, 512], "pa")
-            pa[a, h] = pa_t
-            n = span(512 * h, 512)
-            nc.tensor.matmul_mx(
-                out=pa_t[:], lhsT=uq[:, span(P * a, P)].bitcast(X4), lhsT_scale=us[:, span(P * a, P)],
-                rhs=zq[:, n].bitcast(X4), rhs_scale=zs[:, n], start=True, stop=True,
-            )
-
-        def a_mul(a, h):
-            ro_a = work.tile([P, 512], F32, tag="s2", name="ro", bufs=10)
-            ro[a, h] = ro_a
-            nc.vector.tensor_tensor(out=ro_a[:], in0=pa[a, h][:], in1=rest_b[:, span(512 * h, 512)], op=ALU.mult)
-
-        def a_add(a, h, vector=False):
-            (nc.vector if vector else nc.gpsimd).tensor_tensor(out=ro[a, h][:], in0=ro[a, h][:], in1=brec_b[:, span(512 * h, 512)], op=ALU.add)
-
-        def a_store(a, h):
-            nc.sync.dma_start(out=rec_view[:, a, span(512 * h, 512)], in_=ro[a, h][:])
-
         pt, rt_s, pc, rq = {}, {}, {}, {}
 
         def t_mm(b, j):
@@ -429,7 +341,7 @@ def tile_cache_pool_upproject_f6_kernel(
             )
 
         def t_affine(b, j):
-            r_t = work.tile([P, 512], F32, tag="s2", name="rt_s", bufs=10)
+            r_t = work.tile([P, 512], F32, tag="s2", name="rt_s", bufs=6)
             nc.scalar.activation(out=r_t[:], in_=pt[b, j][:], func=ACT.Identity, scale=cols[:, j : j + 1], bias=cols[:, 8 + j : 9 + j])
             rt_s[b, j] = r_t
 
@@ -452,7 +364,7 @@ def tile_cache_pool_upproject_f6_kernel(
 
         keys_view = keys.rearrange("(m t) e -> m t e", t=4)
         values_view = values.rearrange("(m t) e -> m t e", t=4)
-        pk, kv, m1, m2, pbias, k_o = {}, {}, {}, {}, {}, {}
+        pk, kv, m1, m2 = {}, {}, {}, {}
 
         def kv_mm(tp, h, n):
             pk_t = bank([P, 512], "pk")
@@ -475,51 +387,30 @@ def tile_cache_pool_upproject_f6_kernel(
                 in1=bup_b[:, span(1024 * h + 512 * n, 512)], op0=ALU.mult, op1=ALU.add,
             )
 
-        def v_tau(tp, n):
-            if (tp, 1) not in kv:
-                kv_t = small([P, 1024], F32, "kv")
-                kv[tp, 1] = kv_t
-            nc.scalar.activation(out=kv[tp, 1][:, span(512 * n, 512)], in_=pk[tp, 1, n][:], func=ACT.Copy, scale=tau_f[:, tp : tp + 1])
-
-        def v_bias(tp, n):
-            c = span(512 * n, 512)
-            nc.gpsimd.tensor_tensor(out=kv[tp, 1][:, c], in0=kv[tp, 1][:, c], in1=bup_b[:, span(1024 + 512 * n, 512)], op=ALU.add)
-
-        def kb_mm(tp, n):
-            pb_t = bank([P, 512], "pb")
-            pbias[tp, n] = pb_t
-            nc.tensor.matmul(
-                out=pb_t[:], lhsT=cs_l[:, tp, :], rhs=rot_b[:].rearrange("p h s d -> p (h s d)")[:, span(512 * n, 512)],
-                start=True, stop=True,
+        def k_cos(tp, vector):
+            m1_t = small([P, 1024], F32, "m1")
+            m1[tp] = m1_t
+            (nc.vector if vector else nc.gpsimd).tensor_tensor(
+                out=m1_t[:].rearrange("p (h d) -> p h d", d=HALF), in0=kv[tp, 0][:].rearrange("p (h d) -> p h d", d=HALF),
+                in1=cos_b[:, tp, :].unsqueeze(1).to_broadcast([P, 16, HALF]), op=ALU.mult,
             )
 
-        def k_parts(tp, n):
-            m1_t = work.tile([P, 512], F32, tag="s2", name="m1", bufs=10)
-            m2_t = work.tile([P, 512], F32, tag="s2", name="m2", bufs=10)
-            m1[tp, n], m2[tp, n] = m1_t, m2_t
-            nc.vector.tensor_tensor(
-                out=m1_t[:].rearrange("p (h d) -> p h d", d=HALF), in0=pk[tp, 0, n][:].rearrange("p (h d) -> p h d", d=HALF),
-                in1=ctau[:, tp, :].unsqueeze(1).to_broadcast([P, 8, HALF]), op=ALU.mult,
+        def k_sin(tp, s, vector):
+            if s == 0:
+                m2_t = small([P, 1024], F32, "m2")
+                m2[tp] = m2_t
+            kh = kv[tp, 0][:].rearrange("p (h s d) -> p h s d", s=2, d=HALF)
+            mh = m2[tp][:].rearrange("p (h s d) -> p h s d", s=2, d=HALF)
+            (nc.vector if vector else nc.gpsimd).tensor_tensor(
+                out=mh[:, :, s, :], in0=kh[:, :, 1 - s, :],
+                in1=ssin[:, tp, s, :].unsqueeze(1).to_broadcast([P, 8, HALF]), op=ALU.mult,
             )
-            kh = pk[tp, 0, n][:].rearrange("p (h s d) -> p h s d", s=2, d=HALF)
-            mh = m2_t[:].rearrange("p (h s d) -> p h s d", s=2, d=HALF)
-            for s in range(2):
-                nc.vector.tensor_tensor(
-                    out=mh[:, :, s, :], in0=kh[:, :, 1 - s, :],
-                    in1=stau[:, tp, s, :].unsqueeze(1).to_broadcast([P, 4, HALF]), op=ALU.mult,
-                )
 
-        def k_sum(tp, n):
-            nc.gpsimd.tensor_tensor(out=m1[tp, n][:], in0=m1[tp, n][:], in1=m2[tp, n][:], op=ALU.add)
-
-        def k_bias(tp, n):
-            if tp not in k_o:
-                k_t = small([P, 1024], F32, "k_o")
-                k_o[tp] = k_t
-            nc.vector.tensor_tensor(out=k_o[tp][:, span(512 * n, 512)], in0=pbias[tp, n][:], in1=m1[tp, n][:], op=ALU.add)
+        def k_add(tp, vector):
+            (nc.vector if vector else nc.gpsimd).tensor_tensor(out=m1[tp][:], in0=m1[tp][:], in1=m2[tp][:], op=ALU.add)
 
         def k_store(tp):
-            nc.sync.dma_start(out=keys_view[:, tp, :], in_=k_o[tp][:])
+            nc.sync.dma_start(out=keys_view[:, tp, :], in_=m1[tp][:])
 
         def v_store(tp):
             nc.sync.dma_start(out=values_view[:, tp, :], in_=kv[tp, 1][:])
@@ -527,14 +418,9 @@ def tile_cache_pool_upproject_f6_kernel(
         for h in range(2):
             for t in range(4):
                 x_widen(0, t, t % 2 == 1, 512 * h, 512)
-        early_masks()
-        by_vector = (0, 1, 0, 1)
-        counts = (0, 0, 2, 2)
-        woven = [list(range(sum(counts[:g]), sum(counts[: g + 1]))) for g in range(4)]
-        done = sum(counts)
-        spreads = ((), (), (), (0, 1))
         for hp in range(2):
             pool_turn(0, hp)
+        by_vector = (0, 2, 1, 1)
         for g in range(4):
             nxt = g + 1
             if nxt < 4:
@@ -542,18 +428,20 @@ def tile_cache_pool_upproject_f6_kernel(
                     x_widen(nxt, t, False)
             for hp in range(2):
                 pool_copy(g, hp)
-            if g == 1:
-                turn_rows()
+            if g == 3:
+                for hp in range(2):
+                    un_copy(0, hp)
             if nxt < 4:
                 for hp in range(2):
                     pool_turn(nxt, hp)
-            for i in spreads[g]:
-                spread(i)
-            for b in woven[g]:
-                w_weave(b)
+            if g == 3:
+                for k in range(3):
+                    for h in range(2):
+                        pooled(2, k, h)
+            if g == 2:
+                for hp in range(2):
+                    un_turn(0, hp)
             x_interleave(g, 0, 512)
-            if g == 1:
-                turn_copy()
             if g < 3:
                 x_interleave(g, 512, 512)
             else:
@@ -565,73 +453,57 @@ def tile_cache_pool_upproject_f6_kernel(
                     x_widen(nxt, t, True)
             x_quantize(g, 1)
             pool_quantize(g)
-            for i in spreads[g]:
-                spread_copy(i, i in (0, 9))
-            for tp in range(2):
+            for tp in range(3 if g == 3 else 2):
                 for h in range(2):
                     pooled(tp, g, h)
-            for b in woven[g]:
-                w_copy(b)
 
-        for tp in range(2, 4):
-            for k in range(4):
-                for h in range(2):
-                    pooled(tp, k, h)
+        for k in range(4):
+            for h in range(2):
+                pooled(3, k, h)
+        for b in range(2):
+            w_direct(b, False)
         for tp in range(3):
             c_add(tp, 0)
             c_add(tp, 1)
             c_square(tp)
-        if done > 1:
-            w_quantize(0, 0)
         c_mean(0)
         c_root(0)
-        un_turn(0, 0)
-        un_turn(0, 1)
+        un_turn(1, 0)
+        un_turn(1, 1)
+        un_turn(2, 0)
+        un_turn(2, 1)
+        turn_rows()
         c_add(3, 0)
         c_add(3, 1)
         c_square(3)
+        un_copy(1, 0)
+        un_copy(1, 1)
         c_scale(0)
         z_make(0)
         z_turn(0)
-        un_copy(0, 0)
-        z_make(1)
-        z_turn(1)
-        un_copy(0, 1)
         c_mean(1)
         c_root(1)
+        z_make(1)
+        z_turn(1)
         un_quantize(0)
-        un_turn(1, 0)
-        un_turn(1, 1)
         c_scale(1)
         z_copy(0)
         z_copy(1)
         z_make(2)
         z_turn(2)
-        un_copy(1, 0)
-        un_copy(1, 1)
-        for i in range(1, done // 2):
-            w_quantize(i // 2, i % 2)
+        un_copy(2, 0)
+        un_copy(2, 1)
         z_make(3)
         z_turn(3)
         zi_interleave(768, 256, False)
         zi_interleave(0, 256)
         zi_interleave(256, 256)
-        z_quantize(0)
         zi_quantize(0, 512)
         zi_interleave(512, 256)
         z_copy(2)
         z_copy(3)
-        z_quantize(1)
+        turn_copy()
         zi_quantize(512, 512)
-        for i in (2, 3, 4):
-            spread(i)
-            spread_copy(i, i in (0, 9))
-        tau_tables()
-        cs_turn()
-        cs_copy()
-        un_quantize(1)
-        z_quantize(2)
-        z_quantize(3)
 
         plan = {}
 
@@ -641,25 +513,11 @@ def tile_cache_pool_upproject_f6_kernel(
                 for s, step in enumerate(job):
                     plan.setdefault((at + s, s != turn), []).append(step)
 
-        def a_job(a, h, vector):
-            def finish():
-                a_mul(a, h)
-                if not vector:
-                    a_add(a, h)
-                    a_store(a, h)
-            def late():
-                if vector:
-                    a_add(a, h, True)
-                    a_store(a, h)
-            return [lambda: a_mm(a, h), finish, late]
-
         def w_job(b):
             def finish():
                 if b % 2 == 1:
                     w_quantize(b // 4, b % 4 // 2)
-            if b in (13, 99):
-                return [lambda: w_direct(b, True), lambda: None, finish]
-            return [lambda: w_weave(b), lambda: w_copy(b), finish]
+            return [lambda: w_direct(b, b not in (99, 99)), finish]
 
         def t_job(units):
             def each(fn):
@@ -669,7 +527,7 @@ def tile_cache_pool_upproject_f6_kernel(
                 return run
             def finish():
                 for b, j in units:
-                    t_copy(b, j, j % 8 in (7, 9))
+                    t_copy(b, j, 8 * b + j >= 104.958 and j % 2 == 1)
                     if j % 4 == 3:
                         t_store(b, j // 4)
             return [each(t_mm), each(t_affine), each(t_turn), finish]
@@ -681,37 +539,42 @@ def tile_cache_pool_upproject_f6_kernel(
             return [lambda: un_turn(b, hp), lambda: un_copy(b, hp), finish]
 
         def k_job(tp, n):
-            def parts():
-                k_parts(tp, n)
-                k_sum(tp, n)
-            def finish():
-                k_bias(tp, n)
+            v = tp in (0, 3)
+            def scale():
+                kv_scale(tp, 0, n)
                 if n == 1:
+                    k_cos(tp, v)
+            def sin():
+                if n == 1:
+                    k_sin(tp, 0, v)
+                    k_sin(tp, 1, v)
+            def finish():
+                if n == 1:
+                    k_add(tp, v)
                     k_store(tp)
-            return [lambda: kv_mm(tp, 0, n), parts] + [lambda: None] * 2 + [lambda: kb_mm(tp, n), finish]
+            return [lambda: kv_mm(tp, 0, n), scale, sin, finish]
 
         def v_job(tp, n):
             def scale():
-                if (tp, n) in ((9, 9), (9, 9)):
-                    v_tau(tp, n)
-                    v_bias(tp, n)
-                else:
-                    kv_scale(tp, 1, n)
+                kv_scale(tp, 1, n)
                 if n == 1:
                     v_store(tp)
             return [lambda: kv_mm(tp, 1, n), scale]
 
-        by_turn = [(b, jh) for b, jh in ((1, 0), (1, 1), (2, 1), (3, 0), (3, 1))]
-        order = [(a, h) for b in (0, 2, 1, 3) for h in range(2) if (b, h) not in by_turn for a in range(4 * b, 4 * b + 4)]
-        stream(7.5, 0.622, [a_job(a, h, True) for a, h in order[:3]])
-        stream(12.5, 1.184, [a_job(a, h, False) for a, h in order[3:]])
-        stream(1, 1.272, [w_job(b) for b in range(done, 16)])
-        stream(0, 0.296, [u_job(b, hp) for b in range(2, 4) for hp in range(2)], 0)
-        stream(0, 1, [[rot_tables]])
-        units = [(b, j) for b, jh in by_turn for j in range(4 * jh, 4 * jh + 4)]
-        stream(8.5, 2.354, [t_job(units[i : i + 2]) for i in range(0, len(units), 2)], 2)
-        stream(18.5, 1.949, [k_job(tp, n) for tp in range(4) for n in range(2)])
-        stream(16, 0.989, [v_job(tp, n) for tp in range(4) for n in range(2)])
+        def z_job(tp):
+            return [lambda: z_quantize(tp)]
+
+        for i in range(2 // 2):
+            w_quantize(i // 2, i % 2)
+        units = [(b, j) for b in range(4) for j in range(8)]
+        stream(0, 0.2, [[lambda: un_quantize(2)]] + [u_job(3, hp) for hp in range(2)], 0)
+        stream(0, 1, [[lambda: un_quantize(1)]])
+        stream(2.5, 0.682, [w_job(b) for b in range(2, 8)])
+        stream(0, 1.911, [z_job(tp) for tp in range(4)] + [[signed_sine]])
+        stream(9, 0.246, [w_job(b) for b in range(8, 16)])
+        stream(0, 1.5, [t_job(units[i : i + 2]) for i in range(0, 32, 2)], 2)
+        stream(11.5, 1.604, [k_job(tp, n) for tp in range(4) for n in range(2)])
+        stream(16, 0.6, [v_job(tp, n) for tp in range(4) for n in range(2)])
         for key in sorted(plan):
             for step in plan[key]:
                 step()

@@ -7,6 +7,7 @@ T, S, D, E = 2048, 512, 1024, 1024
 HALF = 64
 EPS = 1e-6
 P = 128
+BANK = 512
 FLOPS = 3 * 2 * S * T * D
 
 F32 = mybir.dt.float32
@@ -42,77 +43,80 @@ def tile_cache_pool_upproject_f6_kernel(
             return psum.tile(shape, dtype, tag="bank", name=label)
 
         def big(shape, dtype, label):
-            return work.tile(shape, dtype, tag="s8", name=label, bufs=5, align_bytes=64)
+            return work.tile(shape, dtype, tag="big", name=label, bufs=5, align_bytes=64)
 
         def small(shape, dtype, label):
-            return work.tile(shape, dtype, tag="s4", name=label, bufs=9, align_bytes=64)
+            return work.tile(shape, dtype, tag="small", name=label, bufs=9, align_bytes=64)
+
+        def code_tile(label):
+            return work.tile([P, 1024], U32, tag="codes", name=label, bufs=5, align_bytes=64)
+
+        def scale_tile(label):
+            return work.tile([P, 1024], U8, tag="scales", name=label, bufs=5, align_bytes=64)
 
         def loaded(shape, label):
-            return work.tile(shape, BF16, tag="ld8", name=label, bufs=6, align_bytes=64)
+            return work.tile(shape, BF16, tag="loaded", name=label, bufs=6, align_bytes=64)
 
-        xsc = keep.tile([P, 4, 4], F32, name="xsc")
-        nc.scalar.dma_start(out=xsc[:], in_=x_scale.rearrange("(g p t) o -> p g (t o)", p=P, t=4))
+        x_scales = keep.tile([P, 4, 4], F32, name="x_scales")
+        nc.scalar.dma_start(out=x_scales[:], in_=x_scale.rearrange("(g p t) o -> p g (t o)", p=P, t=4))
         x_view = x_bytes.rearrange("(g p t) d -> g p t d", p=P, t=4)
         pool_view = pool.rearrange("(m t) k -> m t k", t=4)
-        rows = keep.tile([P, P], BF16, name="rows")
-        nc.vector.memset(rows[:], 0.0)
-        xb = []
-        pr = []
-        un = []
-        wr = {}
-        ss_b = keep.tile([P, 4], BF16, name="ss_b")
-        tau_b = keep.tile([P, 4], BF16, name="tau_b")
-        cos_b = keep.tile([P, 4, HALF], BF16, name="cos_b")
-        sin_b = keep.tile([P, 4, HALF], BF16, name="sin_b")
-        emb = keep.tile([P, 4, D], BF16, name="emb")
         un_view = unpool.rearrange("(p a) s -> p a s", a=16)
         w_view = w_up.rearrange("(g p t) n -> g p t n", p=P, t=4)
 
+        rows = keep.tile([P, P], BF16, name="rows")
+        nc.vector.memset(rows[:], 0.0)
+        slot_scales = keep.tile([P, 4], BF16, name="slot_scales")
+        taus = keep.tile([P, 4], BF16, name="taus")
+        cosines = keep.tile([P, 4, HALF], BF16, name="cosines")
+        sines = keep.tile([P, 4, HALF], BF16, name="sines")
+        embeddings = keep.tile([P, 4, D], BF16, name="embeddings")
+        gains = keep.tile([P, D], BF16, name="gains")
+        up_biases = keep.tile([P, 2 * E], BF16, name="up_biases")
+        x_raw, pool_raw, un_raw, w_raw = [], [], [], {}
+
         def load_x(g):
-            xb_g = keep.tile([P, 4, D], U8, name="xb%d" % g, align_bytes=64)
-            for part in range(2 if g == 0 else 1):
-                n = span(2 * part, 2) if g == 0 else span(0, 4)
-                nc.sync.dma_start(out=xb_g[:, n, :], in_=x_view[g][:, n, :])
-            xb.append(xb_g)
+            raw = keep.tile([P, 4, D], U8, name="x_raw%d" % g, align_bytes=64)
+            for n in (span(0, 2), span(2, 2)) if g == 0 else (span(0, 4),):
+                nc.sync.dma_start(out=raw[:, n, :], in_=x_view[g][:, n, :])
+            x_raw.append(raw)
 
         def load_pool(i):
-            pr_i = loaded([P, 4, 1024], "pr")
-            nc.sync.dma_start(out=pr_i[:], in_=pool_view[:, :, span(1024 * i, 1024)])
-            pr.append(pr_i)
+            raw = loaded([P, 4, 1024], "pool_raw")
+            nc.sync.dma_start(out=raw[:], in_=pool_view[:, :, span(1024 * i, 1024)])
+            pool_raw.append(raw)
 
         def load_un(i):
-            un_i = loaded([P, 8, S], "un")
-            nc.sync.dma_start(out=un_i[:], in_=un_view[:, span(8 * i, 8), :])
-            un.append(un_i)
+            raw = loaded([P, 8, S], "un_raw")
+            nc.sync.dma_start(out=raw[:], in_=un_view[:, span(8 * i, 8), :])
+            un_raw.append(raw)
 
         def load_w(q):
-            w_q = loaded([P, 4, 1024], "wr")
-            nc.sync.dma_start(out=w_q[:], in_=w_view[q % 2][:, :, span(1024 * (q // 2), 1024)])
-            wr[q] = w_q
+            raw = loaded([P, 4, 1024], "w_raw")
+            nc.sync.dma_start(out=raw[:], in_=w_view[q % 2][:, :, span(1024 * (q // 2), 1024)])
+            w_raw[q] = raw
 
-        gain_b = keep.tile([P, D], BF16, name="gain_b")
-        bup_b = keep.tile([P, 2 * E], BF16, name="bup_b")
         load_x(0)
         load_x(1)
         load_pool(0)
         load_x(2)
         load_x(3)
         load_pool(1)
-        nc.sync.dma_start(out=ss_b[:], in_=slot_scale.rearrange("(m t) -> m t", t=4))
+        nc.sync.dma_start(out=slot_scales[:], in_=slot_scale.rearrange("(m t) -> m t", t=4))
         nc.sync.dma_start(out=rows[0:8, :], in_=restore.rearrange("(j p) -> j p", p=P))
         nc.sync.dma_start(out=rows[8:16, :], in_=b_rec.rearrange("(j p) -> j p", p=P))
         load_un(0)
-        nc.sync.dma_start(out=emb[:], in_=slot_emb.rearrange("(m t) d -> m t d", t=4))
-        nc.sync.dma_start(out=gain_b[:], in_=gain.partition_broadcast(P))
-        load_w(0)
-        load_un(1)
-        load_w(1)
-        nc.sync.dma_start(out=tau_b[:], in_=tau.rearrange("(m t) -> m t", t=4))
-        nc.sync.dma_start(out=cos_b[:], in_=cos_t.rearrange("(m t) d -> m t d", t=4))
-        nc.sync.dma_start(out=sin_b[:], in_=sin_t.rearrange("(m t) d -> m t d", t=4))
+        nc.sync.dma_start(out=embeddings[:], in_=slot_emb.rearrange("(m t) d -> m t d", t=4))
+        nc.sync.dma_start(out=gains[:], in_=gain.partition_broadcast(P))
         load_w(2)
+        load_un(1)
         load_w(3)
-        nc.sync.dma_start(out=bup_b[:], in_=b_up.partition_broadcast(P))
+        nc.sync.dma_start(out=taus[:], in_=tau.rearrange("(m t) -> m t", t=4))
+        nc.sync.dma_start(out=cosines[:], in_=cos_t.rearrange("(m t) d -> m t d", t=4))
+        nc.sync.dma_start(out=sines[:], in_=sin_t.rearrange("(m t) d -> m t d", t=4))
+        nc.sync.dma_start(out=up_biases[:], in_=b_up.partition_broadcast(P))
+        load_w(0)
+        load_w(1)
 
         one = keep.tile([P, 1], F32, name="one")
         nc.vector.memset(one[:], 1.0)
@@ -122,371 +126,345 @@ def tile_cache_pool_upproject_f6_kernel(
         make_identity(nc, ident[:])
         ident16 = keep.tile([P, P], BF16, name="ident16")
         make_identity(nc, ident16[:])
-        cols = keep.tile([P, 16], F32, name="cols")
-        ssin = keep.tile([P, 4, 2, HALF], BF16, name="ssin")
-        turned = {}
+        columns = keep.tile([P, 16], F32, name="columns")
+        signed_sines = keep.tile([P, 4, 2, HALF], BF16, name="signed_sines")
+        turned_rows = {}
 
-        def turn_rows():
-            turned[0] = bank([P, P], "turned", BF16)
-            nc.tensor.transpose(turned[0][:], rows[:], ident16[:])
+        def rows_turn():
+            turned_rows[0] = bank([P, P], "turned_rows", BF16)
+            nc.tensor.transpose(turned_rows[0][:], rows[:], ident16[:])
 
-        def turn_copy():
-            nc.vector.tensor_copy(out=cols[:], in_=turned[0][:, 0:16])
+        def rows_copy():
+            nc.vector.tensor_copy(out=columns[:], in_=turned_rows[0][:, 0:16])
 
-        def signed_sine():
-            nc.vector.tensor_scalar(out=ssin[:, :, 0, :], in0=sin_b[:], scalar1=-1.0, scalar2=None, op0=ALU.mult)
-            nc.vector.tensor_copy(out=ssin[:, :, 1, :], in_=sin_b[:])
+        def sign_sines():
+            nc.vector.tensor_scalar(out=signed_sines[:, :, 0, :], in0=sines[:], scalar1=-1.0, scalar2=None, op0=ALU.mult)
+            nc.vector.tensor_copy(out=signed_sines[:, :, 1, :], in_=sines[:])
 
-        def interleave(engine_copy, dst, src):
-            engine_copy(
-                out=dst.rearrange("p (c i) t -> p c t i", i=4),
-                in_=src.rearrange("p t (c i) -> p c t i", i=4),
+        def interleave(out, in_, vector=True):
+            copy = nc.vector.tensor_copy if vector else nc.scalar.copy
+            copy(out=out.rearrange("p (c i) t -> p c t i", i=4), in_=in_.rearrange("p t (c i) -> p c t i", i=4))
+
+        def quantize(codes, scales, grouped):
+            nc.vector.quantize_mx(out=codes.bitcast(X4), scales=scales, in_=grouped)
+
+        def transpose_pairs(out, source, base):
+            for u in range(2):
+                nc.tensor.transpose(out[:, u, :], source[:, base + u : base + 256 : 2], ident[:])
+
+        def multiply(out, left, left_scales, right, right_scales, start, stop):
+            nc.tensor.matmul_mx(
+                out=out, lhsT=left.bitcast(X4), lhsT_scale=left_scales, rhs=right.bitcast(X4), rhs_scale=right_scales,
+                start=start, stop=stop,
             )
 
-        def quantize(codes, scales, values4):
-            nc.vector.quantize_mx(out=codes.bitcast(X4), scales=scales, in_=values4)
-
-        xw, xi, xq, xs, pi, pq, ps = {}, {}, {}, {}, {}, {}, {}
-        turned_pool, acc = {}, {}
+        x_wide, x_grouped, x_codes, x_code_scales = {}, {}, {}, {}
+        pool_turned, pool_grouped, pool_codes, pool_code_scales = {}, {}, {}, {}
+        sums = {}
 
         def x_widen(g, t, vector, at=0, width=D):
-            if g not in xw:
-                xw_g = big([P, 4, D], BF16, "xw")
-                xw[g] = xw_g
+            if g not in x_wide:
+                x_wide[g] = big([P, 4, D], BF16, "x_wide")
             c = span(at, width)
-            src = xb[g][:, t, c].bitcast(FP8)
-            scale = xsc[:, g, t : t + 1]
+            source = x_raw[g][:, t, c].bitcast(FP8)
+            scale = x_scales[:, g, t : t + 1]
             if vector:
-                nc.vector.tensor_scalar(out=xw[g][:, t, c], in0=src, scalar1=scale, scalar2=None, op0=ALU.mult)
+                nc.vector.tensor_scalar(out=x_wide[g][:, t, c], in0=source, scalar1=scale, scalar2=None, op0=ALU.mult)
             else:
-                nc.scalar.activation(out=xw[g][:, t, c], in_=src, func=ACT.Copy, scale=scale)
+                nc.scalar.activation(out=x_wide[g][:, t, c], in_=source, func=ACT.Copy, scale=scale)
 
         def x_interleave(g, at, width, vector=True):
-            if g not in xi:
-                xi_g = big([P, D, 4], BF16, "xi")
-                xi[g] = xi_g
+            if g not in x_grouped:
+                x_grouped[g] = big([P, D, 4], BF16, "x_grouped")
             c = span(at, width)
-            interleave(nc.vector.tensor_copy if vector else nc.scalar.copy, xi[g][:, c, :], xw[g][:, :, c])
+            interleave(x_grouped[g][:, c, :], x_wide[g][:, :, c], vector)
 
         def x_quantize(g, h):
-            if g not in xq:
-                xq_g = work.tile([P, 1024], U32, tag="codes", name="xq", bufs=5, align_bytes=64)
-                xs_g = work.tile([P, 1024], U8, tag="scales", name="xs", bufs=5, align_bytes=64)
-                xq[g], xs[g] = xq_g, xs_g
-            c = span(512 * h, 512)
-            quantize(xq[g][:, c], xs[g][:, c], xi[g][:, c, :].rearrange("p c j -> p (c j)"))
+            if g not in x_codes:
+                x_codes[g] = code_tile("x_codes")
+                x_code_scales[g] = scale_tile("x_code_scales")
+            c = span(BANK * h, BANK)
+            quantize(x_codes[g][:, c], x_code_scales[g][:, c], x_grouped[g][:, c, :].rearrange("p c t -> p (c t)"))
 
-        def pool_turn(g, hp):
-            pw = words(pr[g // 2][:].rearrange("m t k -> m (t k)"))
-            tb = bank([P, 2, 2, P], "tb")
-            turned_pool[g, hp] = tb
+        def pool_turn(g, half):
+            source = words(pool_raw[g // 2][:].rearrange("m s k -> m (s k)"))
+            turned = bank([P, 2, 2, P], "pool_turned")
             for i in range(2):
-                base = (2 * hp + i) * 512 + 256 * (g % 2)
-                for u in range(2):
-                    nc.tensor.transpose(tb[:, i, u, :], pw[:, base + u : base + 256 : 2], ident[:])
+                transpose_pairs(turned[:, i], source, 512 * (2 * half + i) + 256 * (g % 2))
+            pool_turned[g, half] = turned
 
-        def pool_copy(g, hp, vector=False):
-            if g not in pi:
-                pi_g = small([P, S, 4], BF16, "pi")
-                pi[g] = pi_g
-            w = words(pi[g][:].rearrange("p c j -> p (c j)")).rearrange("p (t m u) -> p t m u", t=4, u=2)
-            fn = nc.vector.tensor_copy if vector else nc.scalar.copy
-            fn(out=w[:, span(2 * hp, 2)], in_=turned_pool[g, hp][:].rearrange("p t u m -> p t m u"))
+        def pool_copy(g, half):
+            if g not in pool_grouped:
+                pool_grouped[g] = small([P, S, 4], BF16, "pool_grouped")
+            out = words(pool_grouped[g][:].rearrange("p c t -> p (c t)")).rearrange("p (s m u) -> p s m u", s=4, u=2)
+            nc.scalar.copy(out=out[:, span(2 * half, 2)], in_=pool_turned[g, half][:].rearrange("p s u m -> p s m u"))
 
         def pool_quantize(g):
-            pq_g = keep.tile([P, S], U32, name="pq%d" % g, align_bytes=64)
-            ps_g = keep.tile([P, S], U8, name="ps%d" % g, align_bytes=64)
-            quantize(pq_g[:], ps_g[:], pi[g][:].rearrange("p c j -> p (c j)"))
-            pq[g], ps[g] = pq_g, ps_g
+            codes = keep.tile([P, S], U32, name="pool_codes%d" % g, align_bytes=64)
+            scales = keep.tile([P, S], U8, name="pool_code_scales%d" % g, align_bytes=64)
+            quantize(codes[:], scales[:], pool_grouped[g][:].rearrange("p c t -> p (c t)"))
+            pool_codes[g], pool_code_scales[g] = codes, scales
 
-        def pooled(tp, g, h):
-            if g == 0:
-                a_t = bank([P, 512], "acc")
-                acc[tp, h] = a_t
-            nc.tensor.matmul_mx(
-                out=acc[tp, h][:],
-                lhsT=pq[g][:, span(P * tp, P)].bitcast(X4), lhsT_scale=ps[g][:, span(P * tp, P)],
-                rhs=xq[g][:, span(512 * h, 512)].bitcast(X4), rhs_scale=xs[g][:, span(512 * h, 512)],
-                start=(g == 0), stop=(g == 3),
-            )
-
-        zb = keep.tile([P, 4, D], BF16, name="zb", align_bytes=64)
-        zi = {}
-        c_f, zt, zti, ztq, zts = {}, {}, {}, {}, {}
-
-        def c_add(tp, h):
-            if h == 0:
-                c_t = small([P, D], F32, "c")
-                c_f[tp] = c_t
-            n = span(512 * h, 512)
-            nc.vector.tensor_tensor(out=c_f[tp][:, n], in0=acc[tp, h][:], in1=emb[:, tp, n], op=ALU.add)
-
-        ssum = keep.tile([P, 4], F32, name="ssum")
-        ms = keep.tile([P, 4], F32, name="ms")
-        rt = keep.tile([P, 4], F32, name="rt")
-        rr = keep.tile([P, 4], F32, name="rr")
-        rs = keep.tile([P, 4], F32, name="rs")
-
-        def c_square(tp):
-            sq = small([P, D], BF16, "sq")
-            nc.scalar.activation(out=sq[:], in_=c_f[tp][:], func=ACT.Square, accum_out=ssum[:, tp : tp + 1])
-
-        def c_mean(pair):
-            n = span(2 * pair, 2)
-            nc.vector.tensor_scalar(out=ms[:, n], in0=ssum[:, n], scalar1=1.0 / D, scalar2=EPS, op0=ALU.mult, op1=ALU.add)
-
-        def c_root(pair):
-            n = span(2 * pair, 2)
-            nc.scalar.activation(out=rt[:, n], in_=ms[:, n], func=ACT.Sqrt)
-
-        def c_scale(pair):
-            n = span(2 * pair, 2)
-            nc.vector.reciprocal(out=rr[:, n], in_=rt[:, n])
-            nc.vector.tensor_tensor(out=rs[:, n], in0=rr[:, n], in1=ss_b[:, n], op=ALU.mult)
-
-        def z_make(tp):
-            nc.vector.scalar_tensor_tensor(out=zb[:, tp, :], in0=c_f[tp][:], scalar=rs[:, tp : tp + 1], in1=gain_b, op0=ALU.mult, op1=ALU.mult)
-
-        def z_turn(tp):
-            zw = words(zb[:, tp, :])
-            zt_t = bank([P, 2, 2, P], "ztb")
-            for g in range(2):
-                for u in range(2):
-                    nc.tensor.transpose(zt_t[:, g, u, :], zw[:, 256 * g + u : 256 * g + 256 : 2], ident[:])
-            zt[tp] = zt_t
-
-        def z_copy(tp):
-            z_t = small([P, 2, P, 4], BF16, "zti")
-            nc.scalar.copy(
-                out=words(z_t[:].rearrange("p g m j -> p (g m j)")).rearrange("p (g m u) -> p g m u", g=2, u=2),
-                in_=zt[tp][:].rearrange("p g u m -> p g m u"),
-            )
-            zti[tp] = z_t
-
-        def z_quantize(tp):
-            ztq_t = keep.tile([P, 2, P], U32, name="ztq%d" % tp, align_bytes=64)
-            zts_t = keep.tile([P, 2, P], U8, name="zts%d" % tp, align_bytes=64)
-            quantize(ztq_t[:].rearrange("p g m -> p (g m)"), zts_t[:].rearrange("p g m -> p (g m)"), zti[tp][:].rearrange("p g m j -> p (g m j)"))
-            ztq[tp], zts[tp] = ztq_t, zts_t
-
-        zq = keep.tile([P, D], U32, name="zq", align_bytes=64)
-        zs = keep.tile([P, D], U8, name="zs", align_bytes=64)
-
-        def zi_interleave(at, width, vector=True):
-            if 0 not in zi:
-                zi_t = big([P, D, 4], BF16, "zi")
-                zi[0] = zi_t
-            c = span(at, width)
-            interleave(nc.vector.tensor_copy if vector else nc.scalar.copy, zi[0][:, c, :], zb[:, :, c])
-
-        def zi_quantize(at, width):
-            c = span(at, width)
-            quantize(zq[:, c], zs[:, c], zi[0][:, c, :].rearrange("p c j -> p (c j)"))
-
-        uq = keep.tile([P, T], U32, name="uq", align_bytes=64)
-        us = keep.tile([P, T], U8, name="us", align_bytes=64)
-        ui, turned_un = {}, {}
-
-        def un_turn(b, hp):
-            uw = words(un[b // 2][:].rearrange("p a s -> p (a s)"))
-            tb = bank([P, 2, 2, P], "tu")
-            turned_un[b, hp] = tb
-            for i in range(2):
-                base = (4 * (b % 2) + 2 * hp + i) * 256
-                for u in range(2):
-                    nc.tensor.transpose(tb[:, i, u, :], uw[:, base + u : base + 256 : 2], ident[:])
-
-        def un_copy(b, hp, vector=False):
-            if b not in ui:
-                ui_b = small([P, 4, P, 4], BF16, "ui")
-                ui[b] = ui_b
-            w = words(ui[b][:].rearrange("p a m j -> p (a m j)")).rearrange("p (a m u) -> p a m u", a=4, u=2)
-            fn = nc.vector.tensor_copy if vector else nc.scalar.copy
-            fn(out=w[:, span(2 * hp, 2)], in_=turned_un[b, hp][:].rearrange("p a u m -> p a m u"))
-
-        def un_quantize(b):
-            c = span(512 * b, 512)
-            quantize(uq[:, c], us[:, c], ui[b][:].rearrange("p a m j -> p (a m j)"))
-
-        wi, wq, ws = {}, {}, {}
-
-        def w_tile(q):
-            if q not in wi:
-                wi_q = big([P, 1024, 4], BF16, "wi")
-                wi[q] = wi_q
-
-        def w_direct(b, vector=True):
-            q, c = b // 4, span(256 * (b % 4), 256)
-            w_tile(q)
-            interleave(nc.vector.tensor_copy if vector else nc.scalar.copy, wi[q][:, c, :], wr[q][:, :, c])
-
-        def w_quantize(q, h):
-            if q not in wq:
-                wq_q = work.tile([P, 1024], U32, tag="codes", name="wq", bufs=5, align_bytes=64)
-                ws_q = work.tile([P, 1024], U8, tag="scales", name="ws", bufs=5, align_bytes=64)
-                wq[q], ws[q] = wq_q, ws_q
-            c = span(512 * h, 512)
-            quantize(wq[q][:, c], ws[q][:, c], wi[q][:, c, :].rearrange("p c j -> p (c j)"))
-
-        rec_view = rec.rearrange("(p a) d -> p a d", a=16)
-        pt, rt_s, pc, rq = {}, {}, {}, {}
-
-        def t_mm(b, j):
-            pt_t = bank([P, 512], "pt")
-            pt[b, j] = pt_t
-            f, c = span(P * j, P), span(512 * b, 512)
-            nc.tensor.matmul_mx(
-                out=pt_t[:], lhsT=zq[:, f].bitcast(X4), lhsT_scale=zs[:, f],
-                rhs=uq[:, c].bitcast(X4), rhs_scale=us[:, c], start=True, stop=True,
-            )
-
-        def t_affine(b, j):
-            r_t = work.tile([P, 512], F32, tag="s2", name="rt_s", bufs=6)
-            nc.scalar.activation(out=r_t[:], in_=pt[b, j][:], func=ACT.Identity, scale=cols[:, j : j + 1], bias=cols[:, 8 + j : 9 + j])
-            rt_s[b, j] = r_t
-
-        def t_turn(b, j):
-            pc_t = bank([P, 4, P], "pc")
-            for i in range(4):
-                nc.tensor.transpose(pc_t[:, i, :], rt_s[b, j][:, span(P * i, P)], ident[:])
-            pc[b, j] = pc_t
-
-        def t_copy(b, j, vector=False):
-            key = (b, j // 4)
-            if key not in rq:
-                rq_t = big([P, 4, 512], F32, "rq")
-                rq[key] = rq_t
-            fn = nc.vector.tensor_copy if vector else nc.scalar.copy
-            fn(out=rq[key][:, :, span(P * (j % 4), P)], in_=pc[b, j][:])
-
-        def t_store(b, jh):
-            nc.sync.dma_start(out=rec_view[:, span(4 * b, 4), span(512 * jh, 512)], in_=rq[b, jh][:])
-
-        keys_view = keys.rearrange("(m t) e -> m t e", t=4)
-        values_view = values.rearrange("(m t) e -> m t e", t=4)
-        pk, kv, m1, m2 = {}, {}, {}, {}
-
-        def kv_mm(tp, h, n):
-            pk_t = bank([P, 512], "pk")
-            pk[tp, h, n] = pk_t
-            c = span(512 * n, 512)
-            for g in range(2):
-                q = 2 * h + g
-                nc.tensor.matmul_mx(
-                    out=pk_t[:], lhsT=ztq[tp][:, g, :].bitcast(X4), lhsT_scale=zts[tp][:, g, :],
-                    rhs=wq[q][:, c].bitcast(X4), rhs_scale=ws[q][:, c], start=(g == 0), stop=(g == 1),
+        def pool_multiply(s, g):
+            for h in range(2):
+                if g == 0:
+                    sums[s, h] = bank([P, BANK], "sums")
+                r, c = span(P * s, P), span(BANK * h, BANK)
+                multiply(
+                    sums[s, h][:], pool_codes[g][:, r], pool_code_scales[g][:, r],
+                    x_codes[g][:, c], x_code_scales[g][:, c], start=(g == 0), stop=(g == 3),
                 )
 
-        def kv_scale(tp, h, n):
-            if (tp, h) not in kv:
-                kv_t = small([P, 1024], F32, "kv")
-                kv[tp, h] = kv_t
-            c = span(512 * n, 512)
+        z = keep.tile([P, 4, D], BF16, name="z", align_bytes=64)
+        c_tiles, z_turned, z_grouped, zf_codes, zf_scales = {}, {}, {}, {}, {}
+        squares = keep.tile([P, 4], F32, name="squares")
+        means = keep.tile([P, 4], F32, name="means")
+        roots = keep.tile([P, 4], F32, name="roots")
+        inverses = keep.tile([P, 4], F32, name="inverses")
+        factors = keep.tile([P, 4], F32, name="factors")
+
+        def c_add(s):
+            c_tiles[s] = small([P, D], F32, "c")
+            for h in range(2):
+                c = span(BANK * h, BANK)
+                nc.vector.tensor_tensor(out=c_tiles[s][:, c], in0=sums[s, h][:], in1=embeddings[:, s, c], op=ALU.add)
+
+        def c_square(s):
+            unused = small([P, D], BF16, "squared")
+            nc.scalar.activation(out=unused[:], in_=c_tiles[s][:], func=ACT.Square, accum_out=squares[:, s : s + 1])
+
+        def norm_mean(pair):
+            n = span(2 * pair, 2)
+            nc.vector.tensor_scalar(out=means[:, n], in0=squares[:, n], scalar1=1.0 / D, scalar2=EPS, op0=ALU.mult, op1=ALU.add)
+
+        def norm_root(pair):
+            n = span(2 * pair, 2)
+            nc.scalar.activation(out=roots[:, n], in_=means[:, n], func=ACT.Sqrt)
+
+        def norm_factor(pair):
+            n = span(2 * pair, 2)
+            nc.vector.reciprocal(out=inverses[:, n], in_=roots[:, n])
+            nc.vector.tensor_tensor(out=factors[:, n], in0=inverses[:, n], in1=slot_scales[:, n], op=ALU.mult)
+
+        def z_make(s):
             nc.vector.scalar_tensor_tensor(
-                out=kv[tp, h][:, c], in0=pk[tp, h, n][:], scalar=tau_b[:, tp : tp + 1],
-                in1=bup_b[:, span(1024 * h + 512 * n, 512)], op0=ALU.mult, op1=ALU.add,
+                out=z[:, s, :], in0=c_tiles[s][:], scalar=factors[:, s : s + 1], in1=gains[:], op0=ALU.mult, op1=ALU.mult,
             )
 
-        def k_cos(tp, vector):
-            m1_t = small([P, 1024], F32, "m1")
-            m1[tp] = m1_t
-            (nc.vector if vector else nc.gpsimd).tensor_tensor(
-                out=m1_t[:].rearrange("p (h d) -> p h d", d=HALF), in0=kv[tp, 0][:].rearrange("p (h d) -> p h d", d=HALF),
-                in1=cos_b[:, tp, :].unsqueeze(1).to_broadcast([P, 16, HALF]), op=ALU.mult,
+        def z_turn(s):
+            z_turned[s] = bank([P, 2, 2, P], "z_turned")
+            for g in range(2):
+                transpose_pairs(z_turned[s][:, g], words(z[:, s, :]), 256 * g)
+
+        def z_copy(s):
+            z_grouped[s] = small([P, 2, P, 4], BF16, "z_grouped")
+            out = words(z_grouped[s][:].rearrange("p g m t -> p (g m t)")).rearrange("p (g m u) -> p g m u", g=2, u=2)
+            nc.scalar.copy(out=out, in_=z_turned[s][:].rearrange("p g u m -> p g m u"))
+
+        def z_quantize(s):
+            codes = keep.tile([P, 2 * P], U32, name="zf_codes%d" % s, align_bytes=64)
+            scales = keep.tile([P, 2 * P], U8, name="zf_scales%d" % s, align_bytes=64)
+            quantize(codes[:], scales[:], z_grouped[s][:].rearrange("p g m t -> p (g m t)"))
+            zf_codes[s], zf_scales[s] = codes, scales
+
+        zs_grouped = {}
+        zs_codes = keep.tile([P, D], U32, name="zs_codes", align_bytes=64)
+        zs_scales = keep.tile([P, D], U8, name="zs_scales", align_bytes=64)
+
+        def zs_interleave(at, vector=True):
+            if 0 not in zs_grouped:
+                zs_grouped[0] = big([P, D, 4], BF16, "zs_grouped")
+            c = span(at, 256)
+            interleave(zs_grouped[0][:, c, :], z[:, :, c], vector)
+
+        def zs_quantize(h):
+            c = span(BANK * h, BANK)
+            quantize(zs_codes[:, c], zs_scales[:, c], zs_grouped[0][:, c, :].rearrange("p c t -> p (c t)"))
+
+        un_codes = keep.tile([P, T], U32, name="un_codes", align_bytes=64)
+        un_scales = keep.tile([P, T], U8, name="un_scales", align_bytes=64)
+        un_turned, un_grouped = {}, {}
+
+        def un_turn(b, half):
+            source = words(un_raw[b // 2][:].rearrange("p a s -> p (a s)"))
+            turned = bank([P, 2, 2, P], "un_turned")
+            for i in range(2):
+                transpose_pairs(turned[:, i], source, 256 * (4 * (b % 2) + 2 * half + i))
+            un_turned[b, half] = turned
+
+        def un_copy(b, half):
+            if b not in un_grouped:
+                un_grouped[b] = small([P, 4, P, 4], BF16, "un_grouped")
+            out = words(un_grouped[b][:].rearrange("p a m t -> p (a m t)")).rearrange("p (a m u) -> p a m u", a=4, u=2)
+            nc.scalar.copy(out=out[:, span(2 * half, 2)], in_=un_turned[b, half][:].rearrange("p a u m -> p a m u"))
+
+        def un_quantize(b):
+            c = span(BANK * b, BANK)
+            quantize(un_codes[:, c], un_scales[:, c], un_grouped[b][:].rearrange("p a m t -> p (a m t)"))
+
+        w_grouped, w_codes, w_code_scales = {}, {}, {}
+
+        def w_interleave(q, quarter, vector=True):
+            if q not in w_grouped:
+                w_grouped[q] = big([P, 1024, 4], BF16, "w_grouped")
+            c = span(256 * quarter, 256)
+            interleave(w_grouped[q][:, c, :], w_raw[q][:, :, c], vector)
+
+        def w_quantize(q, h):
+            if q not in w_codes:
+                w_codes[q] = code_tile("w_codes")
+                w_code_scales[q] = scale_tile("w_code_scales")
+            c = span(BANK * h, BANK)
+            quantize(w_codes[q][:, c], w_code_scales[q][:, c], w_grouped[q][:, c, :].rearrange("p c t -> p (c t)"))
+
+        rec_view = rec.rearrange("(p a) d -> p a d", a=16)
+        rec_product, rec_scaled, rec_turned, rec_out = {}, {}, {}, {}
+
+        def rec_multiply(b, j):
+            rec_product[b, j] = bank([P, BANK], "rec_product")
+            f, c = span(P * j, P), span(BANK * b, BANK)
+            multiply(
+                rec_product[b, j][:], zs_codes[:, f], zs_scales[:, f], un_codes[:, c], un_scales[:, c],
+                start=True, stop=True,
             )
 
-        def k_sin(tp, s, vector):
-            if s == 0:
-                m2_t = small([P, 1024], F32, "m2")
-                m2[tp] = m2_t
-            kh = kv[tp, 0][:].rearrange("p (h s d) -> p h s d", s=2, d=HALF)
-            mh = m2[tp][:].rearrange("p (h s d) -> p h s d", s=2, d=HALF)
-            (nc.vector if vector else nc.gpsimd).tensor_tensor(
-                out=mh[:, :, s, :], in0=kh[:, :, 1 - s, :],
-                in1=ssin[:, tp, s, :].unsqueeze(1).to_broadcast([P, 8, HALF]), op=ALU.mult,
+        def rec_scale(b, j):
+            rec_scaled[b, j] = work.tile([P, BANK], F32, tag="scaled", name="rec_scaled", bufs=4)
+            nc.scalar.activation(
+                out=rec_scaled[b, j][:], in_=rec_product[b, j][:], func=ACT.Identity,
+                scale=columns[:, j : j + 1], bias=columns[:, 8 + j : 9 + j],
             )
 
-        def k_add(tp, vector):
-            (nc.vector if vector else nc.gpsimd).tensor_tensor(out=m1[tp][:], in0=m1[tp][:], in1=m2[tp][:], op=ALU.add)
+        def rec_turn(b, j):
+            rec_turned[b, j] = bank([P, 4, P], "rec_turned")
+            for i in range(4):
+                nc.tensor.transpose(rec_turned[b, j][:, i, :], rec_scaled[b, j][:, span(P * i, P)], ident[:])
 
-        def k_store(tp):
-            nc.sync.dma_start(out=keys_view[:, tp, :], in_=m1[tp][:])
+        def rec_copy(b, j):
+            if (b, j // 4) not in rec_out:
+                rec_out[b, j // 4] = big([P, 4, BANK], F32, "rec_out")
+            nc.scalar.copy(out=rec_out[b, j // 4][:, :, span(P * (j % 4), P)], in_=rec_turned[b, j][:])
 
-        def v_store(tp):
-            nc.sync.dma_start(out=values_view[:, tp, :], in_=kv[tp, 1][:])
+        def rec_store(b, j, count):
+            width = P * count
+            nc.sync.dma_start(
+                out=rec_view[:, span(4 * b, 4), span(P * (j + 1) - width, width)],
+                in_=rec_out[b, j // 4][:, :, span(P * (j % 4 + 1) - width, width)],
+            )
+
+        sides = [out.rearrange("(m s) e -> m s e", s=4) for out in (keys, values)]
+        kv_product, kv, rotated, swapped = {}, {}, {}, {}
+
+        def kv_multiply(side, s, h):
+            kv_product[side, s, h] = bank([P, BANK], "kv_product")
+            c = span(BANK * h, BANK)
+            for g in range(2):
+                q, r = 2 * side + g, span(P * g, P)
+                multiply(
+                    kv_product[side, s, h][:], zf_codes[s][:, r], zf_scales[s][:, r],
+                    w_codes[q][:, c], w_code_scales[q][:, c], start=(g == 0), stop=(g == 1),
+                )
+
+        def kv_affine(side, s, h):
+            if (side, s) not in kv:
+                kv[side, s] = small([P, 1024], F32, "kv")
+            nc.vector.scalar_tensor_tensor(
+                out=kv[side, s][:, span(BANK * h, BANK)], in0=kv_product[side, s, h][:], scalar=taus[:, s : s + 1],
+                in1=up_biases[:, span(1024 * side + BANK * h, BANK)], op0=ALU.mult, op1=ALU.add,
+            )
+
+        def value_store(s):
+            nc.sync.dma_start(out=sides[1][:, s, :], in_=kv[1, s][:])
+
+        def key_cosine(s):
+            rotated[s] = small([P, 1024], F32, "rotated")
+            nc.vector.tensor_tensor(
+                out=rotated[s][:].rearrange("p (n d) -> p n d", d=HALF), in0=kv[0, s][:].rearrange("p (n d) -> p n d", d=HALF),
+                in1=cosines[:, s, :].unsqueeze(1).to_broadcast([P, 16, HALF]), op=ALU.mult,
+            )
+
+        def key_sine(s):
+            swapped[s] = small([P, 1024], F32, "swapped")
+            out = swapped[s][:].rearrange("p (n i d) -> p n i d", i=2, d=HALF)
+            in_ = kv[0, s][:].rearrange("p (n i d) -> p n i d", i=2, d=HALF)
+            for i in range(2):
+                nc.vector.tensor_tensor(
+                    out=out[:, :, i, :], in0=in_[:, :, 1 - i, :],
+                    in1=signed_sines[:, s, i, :].unsqueeze(1).to_broadcast([P, 8, HALF]), op=ALU.mult,
+                )
+
+        def key_add(s, at, width):
+            c = span(at, width)
+            nc.vector.tensor_tensor(out=rotated[s][:, c], in0=rotated[s][:, c], in1=swapped[s][:, c], op=ALU.add)
+
+        def key_store(s, at, width):
+            c = span(at, width)
+            nc.sync.dma_start(out=sides[0][:, s, c], in_=rotated[s][:, c])
 
         for h in range(2):
             for t in range(4):
-                x_widen(0, t, t % 2 == 1, 512 * h, 512)
-        for hp in range(2):
-            pool_turn(0, hp)
+                x_widen(0, t, t % 2 == 1, BANK * h, BANK)
+        for half in range(2):
+            pool_turn(0, half)
         by_vector = (0, 2, 1, 1)
         for g in range(4):
             nxt = g + 1
             if nxt < 4:
                 for t in range(4 - by_vector[nxt]):
                     x_widen(nxt, t, False)
-            for hp in range(2):
-                pool_copy(g, hp)
+            for half in range(2):
+                pool_copy(g, half)
             if g == 3:
-                for hp in range(2):
-                    un_copy(0, hp)
+                for half in range(2):
+                    un_copy(0, half)
             if nxt < 4:
-                for hp in range(2):
-                    pool_turn(nxt, hp)
+                for half in range(2):
+                    pool_turn(nxt, half)
+            if g == 2:
+                for half in range(2):
+                    un_turn(0, half)
             if g == 3:
                 for k in range(3):
-                    for h in range(2):
-                        pooled(2, k, h)
-            if g == 2:
-                for hp in range(2):
-                    un_turn(0, hp)
-            x_interleave(g, 0, 512)
-            if g < 3:
-                x_interleave(g, 512, 512)
+                    pool_multiply(2, k)
+            x_interleave(g, 0, BANK)
+            if nxt < 4:
+                x_interleave(g, BANK, BANK)
             else:
                 x_interleave(g, 768, 256, False)
-                x_interleave(g, 512, 256)
+                x_interleave(g, BANK, 256)
             x_quantize(g, 0)
             if nxt < 4:
                 for t in range(4 - by_vector[nxt], 4):
                     x_widen(nxt, t, True)
             x_quantize(g, 1)
             pool_quantize(g)
-            for tp in range(3 if g == 3 else 2):
-                for h in range(2):
-                    pooled(tp, g, h)
-
-        for k in range(4):
-            for h in range(2):
-                pooled(3, k, h)
-        for b in range(2):
-            w_direct(b, False)
-        for tp in range(3):
-            c_add(tp, 0)
-            c_add(tp, 1)
-            c_square(tp)
-        c_mean(0)
-        c_root(0)
-        un_turn(1, 0)
-        un_turn(1, 1)
-        un_turn(2, 0)
-        un_turn(2, 1)
-        turn_rows()
-        c_add(3, 0)
-        c_add(3, 1)
+            for s in range(2 if nxt < 4 else 3):
+                pool_multiply(s, g)
+        for g in range(4):
+            pool_multiply(3, g)
+        for quarter in range(3):
+            w_interleave(2, quarter, False)
+        for s in range(3):
+            c_add(s)
+            c_square(s)
+        norm_mean(0)
+        norm_root(0)
+        for b, half in ((1, 0), (1, 1), (2, 0), (2, 1)):
+            un_turn(b, half)
+        rows_turn()
+        c_add(3)
         c_square(3)
         un_copy(1, 0)
         un_copy(1, 1)
-        c_scale(0)
+        norm_factor(0)
         z_make(0)
         z_turn(0)
-        c_mean(1)
-        c_root(1)
+        norm_mean(1)
+        norm_root(1)
         z_make(1)
         z_turn(1)
         un_quantize(0)
-        c_scale(1)
+        norm_factor(1)
         z_copy(0)
         z_copy(1)
         z_make(2)
@@ -495,86 +473,81 @@ def tile_cache_pool_upproject_f6_kernel(
         un_copy(2, 1)
         z_make(3)
         z_turn(3)
-        zi_interleave(768, 256, False)
-        zi_interleave(0, 256)
-        zi_interleave(256, 256)
-        zi_quantize(0, 512)
-        zi_interleave(512, 256)
+        zs_interleave(768, False)
+        zs_interleave(0)
+        zs_interleave(256)
+        zs_quantize(0)
+        zs_interleave(512)
         z_copy(2)
         z_copy(3)
-        turn_copy()
-        zi_quantize(512, 512)
+        rows_copy()
+        zs_quantize(1)
+        w_quantize(2, 0)
 
-        plan = {}
+        rounds = {}
 
-        def stream(first, pace, jobs, turn=-1):
+        def stream(first, pace, jobs, turning=-1):
             for k, job in enumerate(jobs):
-                at = int(first + pace * k)
-                for s, step in enumerate(job):
-                    plan.setdefault((at + s, s != turn), []).append(step)
+                for n, step in enumerate(job):
+                    rounds.setdefault((int(first + pace * k) + n, n != turning), []).append(step)
 
-        def w_job(b):
+        def un_job(b, half):
             def finish():
-                if b % 2 == 1:
-                    w_quantize(b // 4, b % 4 // 2)
-            return [lambda: w_direct(b, b not in (99, 99)), finish]
+                if half == 1:
+                    un_quantize(b)
+            return [lambda: un_turn(b, half), lambda: un_copy(b, half), finish]
 
-        def t_job(units):
-            def each(fn):
+        def w_job(q, quarter):
+            def finish():
+                if quarter % 2 == 1:
+                    w_quantize(q, quarter // 2)
+            return [lambda: w_interleave(q, quarter, (q, quarter) not in ((3, 3), (9, 9))), finish]
+
+        def rec_job(units):
+            def each(step):
                 def run():
                     for b, j in units:
-                        fn(b, j)
+                        step(b, j)
                 return run
             def finish():
                 for b, j in units:
-                    t_copy(b, j, 8 * b + j >= 104.958 and j % 2 == 1)
-                    if j % 4 == 3:
-                        t_store(b, j // 4)
-            return [each(t_mm), each(t_affine), each(t_turn), finish]
+                    rec_copy(b, j)
+                    if (b, j) in stores:
+                        rec_store(b, j, stores[b, j])
+            return [each(rec_multiply), each(rec_scale), each(rec_turn), finish]
 
-        def u_job(b, hp):
+        def kv_job(side, s, h):
             def finish():
-                if hp == 1:
-                    un_quantize(b)
-            return [lambda: un_turn(b, hp), lambda: un_copy(b, hp), finish]
+                kv_affine(side, s, h)
+                if (side, h) == (1, 1):
+                    value_store(s)
+            return [lambda: kv_multiply(side, s, h), finish]
 
-        def k_job(tp, n):
-            v = tp in (0, 3)
-            def scale():
-                kv_scale(tp, 0, n)
-                if n == 1:
-                    k_cos(tp, v)
-            def sin():
-                if n == 1:
-                    k_sin(tp, 0, v)
-                    k_sin(tp, 1, v)
-            def finish():
-                if n == 1:
-                    k_add(tp, v)
-                    k_store(tp)
-            return [lambda: kv_mm(tp, 0, n), scale, sin, finish]
+        def key_job(s):
+            parts = [(0, 1024)] if s < 3 else [(0, 512), (512, 512)]
+            def add(n):
+                return lambda: key_add(s, *parts[n])
+            def store(n):
+                return lambda: key_store(s, *parts[n])
+            job = [lambda: key_cosine(s), lambda: key_sine(s)]
+            for n in range(len(parts)):
+                job += [add(n), store(n)]
+            return job
 
-        def v_job(tp, n):
-            def scale():
-                kv_scale(tp, 1, n)
-                if n == 1:
-                    v_store(tp)
-            return [lambda: kv_mm(tp, 1, n), scale]
-
-        def z_job(tp):
-            return [lambda: z_quantize(tp)]
-
-        for i in range(2 // 2):
-            w_quantize(i // 2, i % 2)
         units = [(b, j) for b in range(4) for j in range(8)]
-        stream(0, 0.2, [[lambda: un_quantize(2)]] + [u_job(3, hp) for hp in range(2)], 0)
-        stream(0, 1, [[lambda: un_quantize(1)]])
-        stream(2.5, 0.682, [w_job(b) for b in range(2, 8)])
-        stream(0, 1.911, [z_job(tp) for tp in range(4)] + [[signed_sine]])
-        stream(9, 0.246, [w_job(b) for b in range(8, 16)])
-        stream(0, 1.5, [t_job(units[i : i + 2]) for i in range(0, 32, 2)], 2)
-        stream(11.5, 1.604, [k_job(tp, n) for tp in range(4) for n in range(2)])
-        stream(16, 0.6, [v_job(tp, n) for tp in range(4) for n in range(2)])
-        for key in sorted(plan):
-            for step in plan[key]:
+        stores = {(b, j): 4 for b, j in units if j % 4 == 3}
+        stores[3, 5] = stores[3, 7] = 2
+        slot_halves = [(s, h) for s in range(4) for h in range(2)]
+        chunk_quarters = [(q, quarter) for q in (2, 3, 0, 1) for quarter in range(4)]
+        stream(4.5, 0.3, [[lambda: un_quantize(2)]] + [un_job(3, half) for half in range(2)], 0)
+        stream(4.5, 1, [[lambda: un_quantize(1)]])
+        stream(0, 0.33, [w_job(q, quarter) for q, quarter in chunk_quarters[3:8]])
+        stream(0, 0.33, [[lambda s=s: z_quantize(s)] for s in range(4)] + [[sign_sines]])
+        stream(7, 0.8, [w_job(q, quarter) for q, quarter in chunk_quarters[8:]])
+        stream(0, 1.5, [rec_job(units[i : i + 2]) for i in range(0, 32, 2)], 2)
+        stream(12.5, 1.25, [kv_job(0, s, h) for s, h in slot_halves])
+        stream(5, 1, [kv_job(1, s, h) for s, h in slot_halves])
+        stream(14.5, 2.7, [key_job(s) for s in range(4)])
+        for key in sorted(rounds):
+            for step in rounds[key]:
                 step()

from contextlib import ExitStack

import concourse.mybir as mybir
from concourse.masks import make_identity

T, S, D, E = 2048, 512, 1024, 1024
HALF = 64
EPS = 1e-6
P = 128
BANK = 512
FLOPS = 3 * 2 * S * T * D

F32 = mybir.dt.float32
BF16 = mybir.dt.bfloat16
U32 = mybir.dt.uint32
U8 = mybir.dt.uint8
FP8 = mybir.dt.float8_e4m3fn
X4 = mybir.dt.float8_e4m3fn_x4
ALU = mybir.AluOpType
ACT = mybir.ActivationFunctionType


def span(start, width):
    return slice(start, start + width)


def words(ap):
    return ap.bitcast(F32)


def tile_cache_pool_upproject_f6_kernel(
    tc, x_bytes, x_scale, pool, slot_emb, gain, slot_scale, w_up, tau, b_up,
    cos_t, sin_t, unpool, restore, b_rec, keys, values, rec,
):
    nc = tc.nc
    with ExitStack() as ctx:
        keep = ctx.enter_context(tc.tile_pool(name="keep", bufs=1))
        work = ctx.enter_context(tc.tile_pool(name="work", bufs=1))
        psum = ctx.enter_context(tc.psum_pool(name="psum", bufs=8))
        ctx.enter_context(tc.manual_schedule())

        def bank(shape, label, dtype=F32):
            return psum.tile(shape, dtype, tag="bank", name=label)

        def big(shape, dtype, label):
            return work.tile(shape, dtype, tag="big", name=label, bufs=5, align_bytes=64)

        def small(shape, dtype, label):
            return work.tile(shape, dtype, tag="small", name=label, bufs=9, align_bytes=64)

        def code_tile(label):
            return work.tile([P, 1024], U32, tag="codes", name=label, bufs=5, align_bytes=64)

        def scale_tile(label):
            return work.tile([P, 1024], U8, tag="scales", name=label, bufs=5, align_bytes=64)

        def loaded(shape, label):
            return work.tile(shape, BF16, tag="loaded", name=label, bufs=6, align_bytes=64)

        x_scales = keep.tile([P, 4, 4], F32, name="x_scales")
        nc.scalar.dma_start(out=x_scales[:], in_=x_scale.rearrange("(g p t) o -> p g (t o)", p=P, t=4))
        x_view = x_bytes.rearrange("(g p t) d -> g p t d", p=P, t=4)
        pool_view = pool.rearrange("(m t) k -> m t k", t=4)
        un_view = unpool.rearrange("(p a) s -> p a s", a=16)
        w_view = w_up.rearrange("(g p t) n -> g p t n", p=P, t=4)

        rows = keep.tile([P, P], BF16, name="rows")
        nc.vector.memset(rows[:], 0.0)
        slot_scales = keep.tile([P, 4], BF16, name="slot_scales")
        taus = keep.tile([P, 4], BF16, name="taus")
        cosines = keep.tile([P, 4, HALF], BF16, name="cosines")
        sines = keep.tile([P, 4, HALF], BF16, name="sines")
        embeddings = keep.tile([P, 4, D], BF16, name="embeddings")
        gains = keep.tile([P, D], BF16, name="gains")
        up_biases = keep.tile([P, 2 * E], BF16, name="up_biases")
        x_raw, pool_raw, un_raw, w_raw = [], [], [], {}

        def load_x(g):
            raw = keep.tile([P, 4, D], U8, name="x_raw%d" % g, align_bytes=64)
            for n in (span(0, 2), span(2, 2)) if g == 0 else (span(0, 4),):
                nc.sync.dma_start(out=raw[:, n, :], in_=x_view[g][:, n, :])
            x_raw.append(raw)

        def load_pool(i):
            raw = loaded([P, 4, 1024], "pool_raw")
            nc.sync.dma_start(out=raw[:], in_=pool_view[:, :, span(1024 * i, 1024)])
            pool_raw.append(raw)

        def load_un(i):
            raw = loaded([P, 8, S], "un_raw")
            nc.sync.dma_start(out=raw[:], in_=un_view[:, span(8 * i, 8), :])
            un_raw.append(raw)

        def load_w(q):
            raw = loaded([P, 4, 1024], "w_raw")
            nc.sync.dma_start(out=raw[:], in_=w_view[q % 2][:, :, span(1024 * (q // 2), 1024)])
            w_raw[q] = raw

        load_x(0)
        load_x(1)
        load_pool(0)
        load_x(2)
        load_x(3)
        load_pool(1)
        nc.sync.dma_start(out=slot_scales[:], in_=slot_scale.rearrange("(m t) -> m t", t=4))
        nc.sync.dma_start(out=rows[0:8, :], in_=restore.rearrange("(j p) -> j p", p=P))
        nc.sync.dma_start(out=rows[8:16, :], in_=b_rec.rearrange("(j p) -> j p", p=P))
        load_un(0)
        nc.sync.dma_start(out=embeddings[:], in_=slot_emb.rearrange("(m t) d -> m t d", t=4))
        nc.sync.dma_start(out=gains[:], in_=gain.partition_broadcast(P))
        load_w(2)
        load_un(1)
        load_w(3)
        nc.sync.dma_start(out=taus[:], in_=tau.rearrange("(m t) -> m t", t=4))
        nc.sync.dma_start(out=cosines[:], in_=cos_t.rearrange("(m t) d -> m t d", t=4))
        nc.sync.dma_start(out=sines[:], in_=sin_t.rearrange("(m t) d -> m t d", t=4))
        nc.sync.dma_start(out=up_biases[:], in_=b_up.partition_broadcast(P))
        load_w(0)
        load_w(1)

        one = keep.tile([P, 1], F32, name="one")
        nc.vector.memset(one[:], 1.0)
        warm = keep.tile([P, 1], F32, name="warm")
        nc.scalar.activation(out=warm[:], in_=one[:], func=ACT.Sqrt)
        ident = keep.tile([P, P], F32, name="ident")
        make_identity(nc, ident[:])
        ident16 = keep.tile([P, P], BF16, name="ident16")
        make_identity(nc, ident16[:])
        columns = keep.tile([P, 16], F32, name="columns")
        signed_sines = keep.tile([P, 4, 2, HALF], BF16, name="signed_sines")
        turned_rows = {}

        def rows_turn():
            turned_rows[0] = bank([P, P], "turned_rows", BF16)
            nc.tensor.transpose(turned_rows[0][:], rows[:], ident16[:])

        def rows_copy():
            nc.vector.tensor_copy(out=columns[:], in_=turned_rows[0][:, 0:16])

        def sign_sines():
            nc.vector.tensor_scalar(out=signed_sines[:, :, 0, :], in0=sines[:], scalar1=-1.0, scalar2=None, op0=ALU.mult)
            nc.vector.tensor_copy(out=signed_sines[:, :, 1, :], in_=sines[:])

        def interleave(out, in_, vector=True):
            copy = nc.vector.tensor_copy if vector else nc.scalar.copy
            copy(out=out.rearrange("p (c i) t -> p c t i", i=4), in_=in_.rearrange("p t (c i) -> p c t i", i=4))

        def quantize(codes, scales, grouped):
            nc.vector.quantize_mx(out=codes.bitcast(X4), scales=scales, in_=grouped)

        def transpose_pairs(out, source, base):
            for u in range(2):
                nc.tensor.transpose(out[:, u, :], source[:, base + u : base + 256 : 2], ident[:])

        def multiply(out, left, left_scales, right, right_scales, start, stop):
            nc.tensor.matmul_mx(
                out=out, lhsT=left.bitcast(X4), lhsT_scale=left_scales, rhs=right.bitcast(X4), rhs_scale=right_scales,
                start=start, stop=stop,
            )

        x_wide, x_grouped, x_codes, x_code_scales = {}, {}, {}, {}
        pool_turned, pool_grouped, pool_codes, pool_code_scales = {}, {}, {}, {}
        sums = {}

        def x_widen(g, t, vector, at=0, width=D):
            if g not in x_wide:
                x_wide[g] = big([P, 4, D], BF16, "x_wide")
            c = span(at, width)
            source = x_raw[g][:, t, c].bitcast(FP8)
            scale = x_scales[:, g, t : t + 1]
            if vector:
                nc.vector.tensor_scalar(out=x_wide[g][:, t, c], in0=source, scalar1=scale, scalar2=None, op0=ALU.mult)
            else:
                nc.scalar.activation(out=x_wide[g][:, t, c], in_=source, func=ACT.Copy, scale=scale)

        def x_interleave(g, at, width, vector=True):
            if g not in x_grouped:
                x_grouped[g] = big([P, D, 4], BF16, "x_grouped")
            c = span(at, width)
            interleave(x_grouped[g][:, c, :], x_wide[g][:, :, c], vector)

        def x_quantize(g, h):
            if g not in x_codes:
                x_codes[g] = code_tile("x_codes")
                x_code_scales[g] = scale_tile("x_code_scales")
            c = span(BANK * h, BANK)
            quantize(x_codes[g][:, c], x_code_scales[g][:, c], x_grouped[g][:, c, :].rearrange("p c t -> p (c t)"))

        def pool_turn(g, half):
            source = words(pool_raw[g // 2][:].rearrange("m s k -> m (s k)"))
            turned = bank([P, 2, 2, P], "pool_turned")
            for i in range(2):
                transpose_pairs(turned[:, i], source, 512 * (2 * half + i) + 256 * (g % 2))
            pool_turned[g, half] = turned

        def pool_copy(g, half):
            if g not in pool_grouped:
                pool_grouped[g] = small([P, S, 4], BF16, "pool_grouped")
            out = words(pool_grouped[g][:].rearrange("p c t -> p (c t)")).rearrange("p (s m u) -> p s m u", s=4, u=2)
            nc.scalar.copy(out=out[:, span(2 * half, 2)], in_=pool_turned[g, half][:].rearrange("p s u m -> p s m u"))

        def pool_quantize(g):
            codes = keep.tile([P, S], U32, name="pool_codes%d" % g, align_bytes=64)
            scales = keep.tile([P, S], U8, name="pool_code_scales%d" % g, align_bytes=64)
            quantize(codes[:], scales[:], pool_grouped[g][:].rearrange("p c t -> p (c t)"))
            pool_codes[g], pool_code_scales[g] = codes, scales

        def pool_multiply(s, g):
            for h in range(2):
                if g == 0:
                    sums[s, h] = bank([P, BANK], "sums")
                r, c = span(P * s, P), span(BANK * h, BANK)
                multiply(
                    sums[s, h][:], pool_codes[g][:, r], pool_code_scales[g][:, r],
                    x_codes[g][:, c], x_code_scales[g][:, c], start=(g == 0), stop=(g == 3),
                )

        z = keep.tile([P, 4, D], BF16, name="z", align_bytes=64)
        c_tiles, z_turned, z_grouped, zf_codes, zf_scales = {}, {}, {}, {}, {}
        squares = keep.tile([P, 4], F32, name="squares")
        means = keep.tile([P, 4], F32, name="means")
        roots = keep.tile([P, 4], F32, name="roots")
        inverses = keep.tile([P, 4], F32, name="inverses")
        factors = keep.tile([P, 4], F32, name="factors")

        def c_add(s):
            c_tiles[s] = small([P, D], F32, "c")
            for h in range(2):
                c = span(BANK * h, BANK)
                nc.vector.tensor_tensor(out=c_tiles[s][:, c], in0=sums[s, h][:], in1=embeddings[:, s, c], op=ALU.add)

        def c_square(s):
            unused = small([P, D], BF16, "squared")
            nc.scalar.activation(out=unused[:], in_=c_tiles[s][:], func=ACT.Square, accum_out=squares[:, s : s + 1])

        def norm_mean(pair):
            n = span(2 * pair, 2)
            nc.vector.tensor_scalar(out=means[:, n], in0=squares[:, n], scalar1=1.0 / D, scalar2=EPS, op0=ALU.mult, op1=ALU.add)

        def norm_root(pair):
            n = span(2 * pair, 2)
            nc.scalar.activation(out=roots[:, n], in_=means[:, n], func=ACT.Sqrt)

        def norm_factor(pair):
            n = span(2 * pair, 2)
            nc.vector.reciprocal(out=inverses[:, n], in_=roots[:, n])
            nc.vector.tensor_tensor(out=factors[:, n], in0=inverses[:, n], in1=slot_scales[:, n], op=ALU.mult)

        def z_make(s):
            nc.vector.scalar_tensor_tensor(
                out=z[:, s, :], in0=c_tiles[s][:], scalar=factors[:, s : s + 1], in1=gains[:], op0=ALU.mult, op1=ALU.mult,
            )

        def z_turn(s):
            z_turned[s] = bank([P, 2, 2, P], "z_turned")
            for g in range(2):
                transpose_pairs(z_turned[s][:, g], words(z[:, s, :]), 256 * g)

        def z_copy(s):
            z_grouped[s] = small([P, 2, P, 4], BF16, "z_grouped")
            out = words(z_grouped[s][:].rearrange("p g m t -> p (g m t)")).rearrange("p (g m u) -> p g m u", g=2, u=2)
            nc.scalar.copy(out=out, in_=z_turned[s][:].rearrange("p g u m -> p g m u"))

        def z_quantize(s):
            codes = keep.tile([P, 2 * P], U32, name="zf_codes%d" % s, align_bytes=64)
            scales = keep.tile([P, 2 * P], U8, name="zf_scales%d" % s, align_bytes=64)
            quantize(codes[:], scales[:], z_grouped[s][:].rearrange("p g m t -> p (g m t)"))
            zf_codes[s], zf_scales[s] = codes, scales

        zs_grouped = {}
        zs_codes = keep.tile([P, D], U32, name="zs_codes", align_bytes=64)
        zs_scales = keep.tile([P, D], U8, name="zs_scales", align_bytes=64)

        def zs_interleave(at, vector=True):
            if 0 not in zs_grouped:
                zs_grouped[0] = big([P, D, 4], BF16, "zs_grouped")
            c = span(at, 256)
            interleave(zs_grouped[0][:, c, :], z[:, :, c], vector)

        def zs_quantize(h):
            c = span(BANK * h, BANK)
            quantize(zs_codes[:, c], zs_scales[:, c], zs_grouped[0][:, c, :].rearrange("p c t -> p (c t)"))

        un_codes = keep.tile([P, T], U32, name="un_codes", align_bytes=64)
        un_scales = keep.tile([P, T], U8, name="un_scales", align_bytes=64)
        un_turned, un_grouped = {}, {}

        def un_turn(b, half):
            source = words(un_raw[b // 2][:].rearrange("p a s -> p (a s)"))
            turned = bank([P, 2, 2, P], "un_turned")
            for i in range(2):
                transpose_pairs(turned[:, i], source, 256 * (4 * (b % 2) + 2 * half + i))
            un_turned[b, half] = turned

        def un_copy(b, half):
            if b not in un_grouped:
                un_grouped[b] = small([P, 4, P, 4], BF16, "un_grouped")
            out = words(un_grouped[b][:].rearrange("p a m t -> p (a m t)")).rearrange("p (a m u) -> p a m u", a=4, u=2)
            nc.scalar.copy(out=out[:, span(2 * half, 2)], in_=un_turned[b, half][:].rearrange("p a u m -> p a m u"))

        def un_quantize(b):
            c = span(BANK * b, BANK)
            quantize(un_codes[:, c], un_scales[:, c], un_grouped[b][:].rearrange("p a m t -> p (a m t)"))

        w_grouped, w_codes, w_code_scales = {}, {}, {}

        def w_interleave(q, quarter, vector=True):
            if q not in w_grouped:
                w_grouped[q] = big([P, 1024, 4], BF16, "w_grouped")
            c = span(256 * quarter, 256)
            interleave(w_grouped[q][:, c, :], w_raw[q][:, :, c], vector)

        def w_quantize(q, h):
            if q not in w_codes:
                w_codes[q] = code_tile("w_codes")
                w_code_scales[q] = scale_tile("w_code_scales")
            c = span(BANK * h, BANK)
            quantize(w_codes[q][:, c], w_code_scales[q][:, c], w_grouped[q][:, c, :].rearrange("p c t -> p (c t)"))

        rec_view = rec.rearrange("(p a) d -> p a d", a=16)
        rec_product, rec_scaled, rec_turned, rec_out = {}, {}, {}, {}

        def rec_multiply(b, j):
            rec_product[b, j] = bank([P, BANK], "rec_product")
            f, c = span(P * j, P), span(BANK * b, BANK)
            multiply(
                rec_product[b, j][:], zs_codes[:, f], zs_scales[:, f], un_codes[:, c], un_scales[:, c],
                start=True, stop=True,
            )

        def rec_scale(b, j):
            rec_scaled[b, j] = work.tile([P, BANK], F32, tag="scaled", name="rec_scaled", bufs=4)
            nc.scalar.activation(
                out=rec_scaled[b, j][:], in_=rec_product[b, j][:], func=ACT.Identity,
                scale=columns[:, j : j + 1], bias=columns[:, 8 + j : 9 + j],
            )

        def rec_turn(b, j):
            rec_turned[b, j] = bank([P, 4, P], "rec_turned")
            for i in range(4):
                nc.tensor.transpose(rec_turned[b, j][:, i, :], rec_scaled[b, j][:, span(P * i, P)], ident[:])

        def rec_copy(b, j):
            if (b, j // 4) not in rec_out:
                rec_out[b, j // 4] = big([P, 4, BANK], F32, "rec_out")
            nc.scalar.copy(out=rec_out[b, j // 4][:, :, span(P * (j % 4), P)], in_=rec_turned[b, j][:])

        def rec_store(b, j, count):
            width = P * count
            nc.sync.dma_start(
                out=rec_view[:, span(4 * b, 4), span(P * (j + 1) - width, width)],
                in_=rec_out[b, j // 4][:, :, span(P * (j % 4 + 1) - width, width)],
            )

        sides = [out.rearrange("(m s) e -> m s e", s=4) for out in (keys, values)]
        kv_product, kv, rotated, swapped = {}, {}, {}, {}

        def kv_multiply(side, s, h):
            kv_product[side, s, h] = bank([P, BANK], "kv_product")
            c = span(BANK * h, BANK)
            for g in range(2):
                q, r = 2 * side + g, span(P * g, P)
                multiply(
                    kv_product[side, s, h][:], zf_codes[s][:, r], zf_scales[s][:, r],
                    w_codes[q][:, c], w_code_scales[q][:, c], start=(g == 0), stop=(g == 1),
                )

        def kv_affine(side, s, h):
            if (side, s) not in kv:
                kv[side, s] = small([P, 1024], F32, "kv")
            nc.vector.scalar_tensor_tensor(
                out=kv[side, s][:, span(BANK * h, BANK)], in0=kv_product[side, s, h][:], scalar=taus[:, s : s + 1],
                in1=up_biases[:, span(1024 * side + BANK * h, BANK)], op0=ALU.mult, op1=ALU.add,
            )

        def value_store(s):
            nc.sync.dma_start(out=sides[1][:, s, :], in_=kv[1, s][:])

        def key_cosine(s):
            rotated[s] = small([P, 1024], F32, "rotated")
            nc.vector.tensor_tensor(
                out=rotated[s][:].rearrange("p (n d) -> p n d", d=HALF), in0=kv[0, s][:].rearrange("p (n d) -> p n d", d=HALF),
                in1=cosines[:, s, :].unsqueeze(1).to_broadcast([P, 16, HALF]), op=ALU.mult,
            )

        def key_sine(s):
            swapped[s] = small([P, 1024], F32, "swapped")
            out = swapped[s][:].rearrange("p (n i d) -> p n i d", i=2, d=HALF)
            in_ = kv[0, s][:].rearrange("p (n i d) -> p n i d", i=2, d=HALF)
            for i in range(2):
                nc.vector.tensor_tensor(
                    out=out[:, :, i, :], in0=in_[:, :, 1 - i, :],
                    in1=signed_sines[:, s, i, :].unsqueeze(1).to_broadcast([P, 8, HALF]), op=ALU.mult,
                )

        def key_add(s, at, width):
            c = span(at, width)
            nc.vector.tensor_tensor(out=rotated[s][:, c], in0=rotated[s][:, c], in1=swapped[s][:, c], op=ALU.add)

        def key_store(s, at, width):
            c = span(at, width)
            nc.sync.dma_start(out=sides[0][:, s, c], in_=rotated[s][:, c])

        for h in range(2):
            for t in range(4):
                x_widen(0, t, t % 2 == 1, BANK * h, BANK)
        for half in range(2):
            pool_turn(0, half)
        by_vector = (0, 2, 1, 1)
        for g in range(4):
            nxt = g + 1
            if nxt < 4:
                for t in range(4 - by_vector[nxt]):
                    x_widen(nxt, t, False)
            for half in range(2):
                pool_copy(g, half)
            if g == 3:
                for half in range(2):
                    un_copy(0, half)
            if nxt < 4:
                for half in range(2):
                    pool_turn(nxt, half)
            if g == 2:
                for half in range(2):
                    un_turn(0, half)
            if g == 3:
                for k in range(3):
                    pool_multiply(2, k)
            x_interleave(g, 0, BANK)
            if nxt < 4:
                x_interleave(g, BANK, BANK)
            else:
                x_interleave(g, 768, 256, False)
                x_interleave(g, BANK, 256)
            x_quantize(g, 0)
            if nxt < 4:
                for t in range(4 - by_vector[nxt], 4):
                    x_widen(nxt, t, True)
            x_quantize(g, 1)
            pool_quantize(g)
            for s in range(2 if nxt < 4 else 3):
                pool_multiply(s, g)
        for g in range(4):
            pool_multiply(3, g)
        for quarter in range(3):
            w_interleave(2, quarter, False)
        for s in range(3):
            c_add(s)
            c_square(s)
        norm_mean(0)
        norm_root(0)
        for b, half in ((1, 0), (1, 1), (2, 0), (2, 1)):
            un_turn(b, half)
        rows_turn()
        c_add(3)
        c_square(3)
        un_copy(1, 0)
        un_copy(1, 1)
        norm_factor(0)
        z_make(0)
        z_turn(0)
        norm_mean(1)
        norm_root(1)
        z_make(1)
        z_turn(1)
        un_quantize(0)
        norm_factor(1)
        z_copy(0)
        z_copy(1)
        z_make(2)
        z_turn(2)
        un_copy(2, 0)
        un_copy(2, 1)
        z_make(3)
        z_turn(3)
        zs_interleave(768, False)
        zs_interleave(0)
        zs_interleave(256)
        zs_quantize(0)
        zs_interleave(512)
        z_copy(2)
        z_copy(3)
        rows_copy()
        zs_quantize(1)
        w_quantize(2, 0)

        rounds = {}

        def stream(first, pace, jobs, turning=-1):
            for k, job in enumerate(jobs):
                for n, step in enumerate(job):
                    rounds.setdefault((int(first + pace * k) + n, n != turning), []).append(step)

        def un_job(b, half):
            def finish():
                if half == 1:
                    un_quantize(b)
            return [lambda: un_turn(b, half), lambda: un_copy(b, half), finish]

        def w_job(q, quarter):
            def finish():
                if quarter % 2 == 1:
                    w_quantize(q, quarter // 2)
            return [lambda: w_interleave(q, quarter, (q, quarter) not in ((3, 3), (9, 9))), finish]

        def rec_job(units):
            def each(step):
                def run():
                    for b, j in units:
                        step(b, j)
                return run
            def finish():
                for b, j in units:
                    rec_copy(b, j)
                    if (b, j) in stores:
                        rec_store(b, j, stores[b, j])
            return [each(rec_multiply), each(rec_scale), each(rec_turn), finish]

        def kv_job(side, s, h):
            def finish():
                kv_affine(side, s, h)
                if (side, h) == (1, 1):
                    value_store(s)
            return [lambda: kv_multiply(side, s, h), finish]

        def key_job(s):
            parts = [(0, 1024)] if s < 3 else [(0, 512), (512, 512)]
            def add(n):
                return lambda: key_add(s, *parts[n])
            def store(n):
                return lambda: key_store(s, *parts[n])
            job = [lambda: key_cosine(s), lambda: key_sine(s)]
            for n in range(len(parts)):
                job += [add(n), store(n)]
            return job

        units = [(b, j) for b in range(4) for j in range(8)]
        stores = {(b, j): 4 for b, j in units if j % 4 == 3}
        stores[3, 5] = stores[3, 7] = 2
        slot_halves = [(s, h) for s in range(4) for h in range(2)]
        chunk_quarters = [(q, quarter) for q in (2, 3, 0, 1) for quarter in range(4)]
        stream(4.5, 0.3, [[lambda: un_quantize(2)]] + [un_job(3, half) for half in range(2)], 0)
        stream(4.5, 1, [[lambda: un_quantize(1)]])
        stream(0, 0.33, [w_job(q, quarter) for q, quarter in chunk_quarters[3:8]])
        stream(0, 0.33, [[lambda s=s: z_quantize(s)] for s in range(4)] + [[sign_sines]])
        stream(7, 0.8, [w_job(q, quarter) for q, quarter in chunk_quarters[8:]])
        stream(0, 1.5, [rec_job(units[i : i + 2]) for i in range(0, 32, 2)], 2)
        stream(12.5, 1.25, [kv_job(0, s, h) for s, h in slot_halves])
        stream(5, 1, [kv_job(1, s, h) for s, h in slot_halves])
        stream(14.5, 2.7, [key_job(s) for s in range(4)])
        for key in sorted(rounds):
            for step in rounds[key]:
                step()
